import numpy as np
import ml_dtypes


def mxq(x, axis, fmt="e4m3"):
    dtype, down = {"e4m3": (ml_dtypes.float8_e4m3fn, 7), "e5m2": (ml_dtypes.float8_e5m2, 14)}[fmt]
    v = np.moveaxis(np.asarray(x, np.float32).astype(ml_dtypes.bfloat16).astype(np.float64), axis, -1)
    blocks = v.reshape(v.shape[:-1] + (-1, 32))
    amax = np.abs(blocks).max(-1, keepdims=True)
    byte = np.maximum(np.where(amax > 0, np.frexp(amax)[1] - 1 + 127, 0) - down, 1)
    scale = np.exp2(byte - 127.0)
    codes = (blocks / scale).astype(np.float32).astype(dtype).astype(np.float64)
    return np.moveaxis((codes * scale).reshape(v.shape), -1, axis)


WIDE = False


def mx_kscale(k):
    if not WIDE:
        return np.ones(k)
    levels = np.array([30, -30])
    if k % 512:
        return np.exp2(np.random.permutation(np.resize(levels, k // 32))).repeat(32)
    a = np.empty((k // 512, 16))
    for p in range(k // 512):
        a[p, :8] = np.random.permutation(np.resize(levels, 8))
        for g in range(8):
            far = levels[np.abs(levels - a[p, g]) >= 10]
            a[p, g + 8] = far[np.random.randint(len(far))]
    return np.exp2(a.ravel()).repeat(32)


BF16 = ml_dtypes.bfloat16


def bf(x):
    return np.asarray(x, np.float32).astype(BF16)


def f64(x):
    return np.asarray(x).astype(np.float64)


E2M1 = np.array([0.0, 0.5, 1.0, 1.5, 2.0, 3.0, 4.0, 6.0, -0.0, -0.5, -1.0, -1.5, -2.0, -3.0, -4.0, -6.0])


def pack_weight(w, fmt):
    k, n = w.shape
    w = f64(bf(w)).reshape(k // 32, 32, n)
    amax = np.abs(w).max(1)
    if fmt == "e4m3":
        byte = np.frexp(amax)[1] - 1 + 127 - 7
    else:
        mant, ex = np.frexp(amax / 6.0)
        byte = np.where(mant > 0.5, ex, ex - 1) + 127
    byte = np.clip(np.where(amax > 0, byte, 1), 1, 254)
    scaled = (w * np.exp2(127.0 - byte)[:, None, :]).reshape(k, n).astype(np.float32)
    by_word = np.ascontiguousarray(scaled.reshape(k // 512, 128, 4, n).transpose(0, 1, 3, 2))
    if fmt == "e4m3":
        words = by_word.astype(ml_dtypes.float8_e4m3fn).view(np.uint8)
    else:
        c = by_word.astype(ml_dtypes.float4_e2m1fn).view(np.uint8) & 0xF
        words = c[..., 0::2] | (c[..., 1::2] << 4)
    return np.ascontiguousarray(words), np.ascontiguousarray(byte.astype(np.uint8).reshape(k // 512, 16, n))


def unpack_weight(words, scales, fmt):
    g, p, n, _ = words.shape
    if fmt == "e4m3":
        vals = np.ascontiguousarray(words).view(ml_dtypes.float8_e4m3fn).astype(np.float64)
    else:
        nib = np.empty((g, p, n, 4), np.uint8)
        nib[..., 0::2] = words & 0xF
        nib[..., 1::2] = words >> 4
        vals = E2M1[nib]
    vals = vals * np.repeat(np.exp2(scales.astype(np.float64) - 127.0), 8, axis=1)[..., None]
    return vals.transpose(0, 1, 3, 2).reshape(g * 512, n)
def pack4(w):
    words, scales = pack_weight(w, "e2m1")
    return words.reshape(words.shape[0], 128, -1), scales


def unpack4(words, scales):
    return unpack_weight(words.reshape(words.shape[0], 128, -1, 2), scales, "e2m1")


M, P, C, S = 1024, 1024, 2048, 512


def setup_inputs():
    s, t = mx_kscale(P), mx_kscale(C)
    orders = np.random.standard_normal((M, P)) * s
    inverse = np.random.standard_normal((P, C)) / np.sqrt(P) / s[:, None] * t
    stock = 0.5 * np.abs(np.random.standard_normal((M, C))) * t
    shares = 2.0 * np.random.standard_normal((C, S)) / np.sqrt(C) / t[:, None]
    contract = 0.3 * np.random.standard_normal(S)
    inv_words, inv_scales = pack4(inverse)
    return {"orders": bf(orders),
            "inv_words": inv_words,
            "inv_scales": inv_scales,
            "stock": bf(stock),
            "shares": bf(shares),
            "contract": bf(contract)}


def reference(orders, inv_words, inv_scales, stock, shares, contract):
    inverse = unpack4(inv_words, inv_scales)
    gross = mxq(f64(orders), 1, "e4m3") @ inverse
    net = np.maximum(gross - f64(stock), 0.0)
    load = mxq(net, 1, "e5m2") @ mxq(f64(shares), 0, "e4m3")
    return load + f64(contract)

@@ -1,0 +1,287 @@
+from contextlib import ExitStack
+
+import concourse.mybir as mybir
+from concourse.masks import make_identity
+
+M, K1, C, S = 1024, 1024, 2048, 512
+FLOPS = 2 * M * K1 * C + 2 * M * C * S
+
+F32 = mybir.dt.float32
+BF16 = mybir.dt.bfloat16
+I32 = mybir.dt.int32
+U32 = mybir.dt.uint32
+U8 = mybir.dt.uint8
+E4M3X4 = mybir.dt.float8_e4m3fn_x4
+E5M2X4 = mybir.dt.float8_e5m2_x4
+E2M1X4 = mybir.dt.float4_e2m1fn_x4
+SUB = mybir.AluOpType.subtract
+ADD = mybir.AluOpType.add
+RELU = mybir.ActivationFunctionType.Relu
+
+P = 128
+KP = 512
+MT = M // P
+G1 = K1 // KP
+G2 = C // KP
+N = 512
+QS_AFTER = {1: 0, 3: 1, 5: 2, 6: 3}
+SI_AFTER = {1: (1, 0), 2: (1, 1), 4: (3, 0), 5: (3, 1)}
+
+
+def tile_material_requirements_planning_s9_kernel(tc, orders, inv_words, inv_scales, stock, shares, contract, out):
+    nc = tc.nc
+    with ExitStack() as ctx:
+        keep = ctx.enter_context(tc.tile_pool(name="keep", bufs=1))
+        work = ctx.enter_context(tc.tile_pool(name="work", bufs=3))
+        psum = ctx.enter_context(tc.psum_pool(name="psum", bufs=1))
+        ctx.enter_context(tc.manual_schedule())
+
+        ident = keep.tile([P, P], F32, name="ident")
+        dummy = keep.tile([P, 8], F32, name="dummy")
+        planes = keep.tile([P, G1, C], U8, name="planes", align_bytes=64)
+        inv_sb = [keep.tile([P, G1, 2 * N], U8, name="inv%d" % c, align_bytes=64) for c in range(G2)]
+        ord_sb = [keep.tile([P, K1], BF16, name="ord%d" % i, align_bytes=64) for i in range(MT)]
+        stk_sb = [keep.tile([P, C], BF16, name="stk%d" % i, align_bytes=64) for i in range(MT)]
+        sh_raw = [keep.tile([P, 4, S], BF16, name="shr%d" % g, align_bytes=64) for g in range(G2)]
+        sh_grp = [keep.tile([P, S, 4], BF16, name="shg%d" % g, align_bytes=64) for g in range(G2)]
+        sh_codes = [keep.tile([P, S], U32, name="shc%d" % g, align_bytes=64) for g in range(G2)]
+        sh_scales = [keep.tile([P, S], U8, name="shs%d" % g, align_bytes=64) for g in range(G2)]
+        ord_codes = [keep.tile([P, G1 * P], U32, name="oc%d" % i, align_bytes=64) for i in range(MT)]
+        ord_scales = [keep.tile([P, G1 * P], U8, name="os%d" % i, align_bytes=64) for i in range(MT)]
+        net_codes = [keep.tile([P, G2 * P], U32, name="nc%d" % i, align_bytes=64) for i in range(MT)]
+        net_scales = [keep.tile([P, G2 * P], U8, name="ns%d" % i, align_bytes=64) for i in range(MT)]
+        con_sb = keep.tile([P, S], BF16, name="con", align_bytes=64)
+
+        def load_orders(i):
+            nc.sync.dma_start(out=ord_sb[i][:], in_=orders[i * P : (i + 1) * P, :])
+
+        def load_stock(i, c0=0, c1=C):
+            nc.sync.dma_start(out=stk_sb[i][:, c0:c1], in_=stock[i * P : (i + 1) * P, c0:c1])
+
+        def load_inv(c):
+            nc.sync.dma_start(
+                out=inv_sb[c][:].bitcast(I32),
+                in_=inv_words.rearrange("g p b -> p g b")[:, :, 2 * N * c : 2 * N * (c + 1)].bitcast(I32),
+            )
+
+        def load_shares(g):
+            nc.sync.dma_start(out=sh_raw[g][:], in_=shares[g * KP : (g + 1) * KP, :].rearrange("(p j) s -> p j s", j=4))
+
+        nc.vector.memset(planes[:].rearrange("p g n -> p (g n)").bitcast(I32), 0)
+        nc.vector.memset(dummy[:], 0.0)
+        make_identity(nc, ident[:])
+        nc.scalar.activation(out=dummy[:], in_=dummy[:], func=RELU)
+
+        for g in range(G1):
+            nc.sync.dma_start(out=ord_sb[0][:, g * KP : (g + 1) * KP], in_=orders[0:P, g * KP : (g + 1) * KP])
+        for r in range(4):
+            nc.sync.dma_start(
+                out=planes[r:P:32, :, :].bitcast(I32),
+                in_=inv_scales.rearrange("g (q r) n -> r q g n", r=4)[r].bitcast(I32),
+            )
+        load_orders(1)
+        load_inv(0)
+        load_stock(0, 0, C // 2)
+        load_inv(1)
+        load_orders(2)
+        load_stock(1, 0, C // 2)
+        load_inv(2)
+        load_stock(0, C // 2, C)
+        load_inv(3)
+        load_stock(1, C // 2, C)
+        load_shares(0)
+        load_orders(3)
+        load_stock(2)
+        load_shares(1)
+        load_orders(4)
+        load_stock(3)
+        load_shares(2)
+        load_orders(5)
+        load_stock(4)
+        load_shares(3)
+        load_orders(6)
+        load_stock(5)
+        load_orders(7)
+        load_stock(6)
+        load_stock(7)
+        nc.sync.dma_start(out=con_sb[:], in_=contract.partition_broadcast(P))
+
+        def bank(tag, bufs):
+            return psum.tile([P, N], F32, name=tag, tag=tag, bufs=bufs)
+
+        def turn_orders(i, g, t, slot, width):
+            words = ord_sb[i][:].bitcast(F32)
+            for u in range(2):
+                nc.tensor.transpose(t[:, u * width + slot * P : u * width + (slot + 1) * P], words[:, 256 * g + u : 256 * (g + 1) : 2], ident[:])
+
+        def orders_half(i, g, tag, bufs, engine_copy, grp):
+            t = bank(tag, bufs)
+            turn_orders(i, g, t, 0, P)
+            engine_copy(
+                out=grp[:, g * 512 : (g + 1) * 512].bitcast(F32).rearrange("p (x u) -> p x u", u=2),
+                in_=t[:, 0:256].rearrange("p (u x) -> p x u", u=2),
+            )
+
+        def orders_tile(i, tag, bufs, grp):
+            t = bank(tag, bufs)
+            for g in range(G1):
+                turn_orders(i, g, t, g, 2 * P)
+            nc.scalar.copy(
+                out=grp[:].bitcast(F32).rearrange("p (x u) -> p x u", u=2),
+                in_=t[:].rearrange("p (u x) -> p x u", u=2),
+            )
+
+        def quantize_orders(i, grp, a=0, b=G1):
+            nc.vector.quantize_mx(
+                out=ord_codes[i][:, a * P : b * P].bitcast(E4M3X4),
+                scales=ord_scales[i][:, a * P : b * P],
+                in_=grp[:, a * 512 : b * 512],
+            )
+
+        def first_product(i, c):
+            acc = bank("mm", 5)
+            for g in range(G1):
+                nc.tensor.matmul_mx(
+                    out=acc[:],
+                    lhsT=ord_codes[i][:, g * P : (g + 1) * P].bitcast(E4M3X4),
+                    lhsT_scale=ord_scales[i][:, g * P : (g + 1) * P],
+                    rhs=inv_sb[c][:, g, :].bitcast(E2M1X4),
+                    rhs_scale=planes[:, g, c * N : (c + 1) * N],
+                    start=(g == 0),
+                    stop=(g == G1 - 1),
+                )
+            return acc
+
+        def subtract_stock(i, c, acc, net):
+            nc.vector.tensor_tensor(
+                out=net[:, c * N : (c + 1) * N].rearrange("m (u p e) -> m u p e", u=2, e=2),
+                in0=acc[:].rearrange("m (p u e) -> m u p e", u=2, e=2),
+                in1=stk_sb[i][:, c * N : (c + 1) * N].rearrange("m (p u e) -> m u p e", u=2, e=2),
+                op=SUB,
+            )
+
+        def turn_net(net, h, tag, bufs):
+            t = bank(tag, bufs)
+            words = net[:].bitcast(F32)
+            for cl in range(2):
+                c = 2 * h + cl
+                for u in range(2):
+                    nc.tensor.transpose(t[:, u * 256 + cl * P : u * 256 + (cl + 1) * P], words[:, 256 * c + P * u : 256 * c + P * (u + 1)], ident[:])
+            return t
+
+        def relu_net(t, h, grp, on_vector=False):
+            o = grp[:, h * 1024 : (h + 1) * 1024].rearrange("p (x u e) -> p x u e", u=2, e=2)
+            i = t[:].bitcast(BF16).rearrange("p (u x e) -> p x u e", u=2, e=2)
+            if on_vector:
+                nc.vector.tensor_scalar_max(out=o, in0=i, scalar1=0.0)
+            else:
+                nc.scalar.activation(out=o, in_=i, func=RELU)
+
+        def quantize_net(i, grp, a=0, b=G2):
+            nc.vector.quantize_mx(
+                out=net_codes[i][:, a * P : b * P].bitcast(E5M2X4),
+                scales=net_scales[i][:, a * P : b * P],
+                in_=grp[:, a * 512 : b * 512],
+            )
+
+        def interleave_shares(g, s0, s1, engine):
+            o = sh_grp[g][:, s0:s1, :].rearrange("p (c i) t -> p c t i", i=4)
+            i = sh_raw[g][:, :, s0:s1].rearrange("p t (c i) -> p c t i", i=4)
+            if engine == "act":
+                nc.scalar.copy(out=o, in_=i)
+            else:
+                nc.vector.tensor_copy(out=o, in_=i)
+
+        def quantize_shares(g):
+            nc.vector.quantize_mx(out=sh_codes[g][:].bitcast(E4M3X4), scales=sh_scales[g][:], in_=sh_grp[g][:].rearrange("p s t -> p (s t)"))
+
+        def second_product(i):
+            acc = bank("mm", 5)
+            for n, g in enumerate(range(G2)):
+                nc.tensor.matmul_mx(
+                    out=acc[:],
+                    lhsT=net_codes[i][:, g * P : (g + 1) * P].bitcast(E5M2X4),
+                    lhsT_scale=net_scales[i][:, g * P : (g + 1) * P],
+                    rhs=sh_codes[g][:].bitcast(E4M3X4),
+                    rhs_scale=sh_scales[g][:],
+                    start=(n == 0),
+                    stop=(n == G2 - 1),
+                )
+            return acc
+
+        def add_and_store(i, acc, parts=1):
+            res = work.tile([P, S], F32, name="res", bufs=4)
+            w = S // parts
+            for k in range(parts):
+                nc.vector.tensor_tensor(out=res[:, k * w : (k + 1) * w], in0=acc[:, k * w : (k + 1) * w], in1=con_sb[:, k * w : (k + 1) * w], op=ADD)
+                queue = nc.sync if k % 2 == 0 else nc.scalar
+                queue.dma_start(out=out[i * P : (i + 1) * P, k * w : (k + 1) * w], in_=res[:, k * w : (k + 1) * w])
+
+        og, nets, ng = {}, {}, {}
+
+        def new_og(i):
+            og[i] = work.tile([P, K1], BF16, name="og", align_bytes=64)
+            return og[i]
+
+        new_og(0)
+        orders_half(0, 0, "nt", 2, nc.scalar.copy, og[0])
+        orders_half(0, 1, "nt", 2, nc.vector.tensor_copy, og[0])
+        quantize_orders(0, og[0], 0, 1)
+        quantize_orders(0, og[0], 1, 2)
+        orders_tile(1, "ot", 1, new_og(1))
+        quantize_orders(1, og[1])
+
+        for tiles in ((0, 1), (2,), (3,), (4,), (5,), (6,), (7,)):
+            i = tiles[-1]
+            for x in tiles:
+                nets[x] = work.tile([P, C], BF16, name="net", align_bytes=64)
+            for c in range(G2):
+                for x in tiles:
+                    acc = first_product(x, c)
+                    if x == 1 and c == 0:
+                        orders_tile(2, "ot", 1, new_og(2))
+                        interleave_shares(0, 0, S // 2, "act")
+                        interleave_shares(0, S // 2, S, "act")
+                    if c == 2 and x >= 4:
+                        quantize_net(x - 4, ng[x - 4])
+                    subtract_stock(x, c, acc, nets[x])
+                    if x == 1 and c == 1:
+                        quantize_orders(2, og[2])
+                    if c == 0 and 2 <= x < MT - 1:
+                        quantize_orders(x + 1, og[x + 1])
+                if i == 4 and c == 1:
+                    interleave_shares(2, S // 2, S, "dve")
+            if i == 3:
+                interleave_shares(2, 0, S // 2, "dve")
+            if i in QS_AFTER:
+                quantize_shares(QS_AFTER[i])
+            accs = [(n, second_product(n)) for n in (range(3) if i == MT - 1 else ())]
+            if i + 2 < MT:
+                orders_tile(i + 2, "ot", 1, new_og(i + 2))
+            ng[i - 1] = work.tile([P, C], BF16, name="ng", align_bytes=64, bufs=5)
+            for h in range(2):
+                t = turn_net(nets[i - 1], h, "nt", 2)
+                relu_net(t, h, ng[i - 1], on_vector=(i == 1 and h == 0))
+            if i in SI_AFTER:
+                g, h = SI_AFTER[i]
+                interleave_shares(g, h * S // 2, (h + 1) * S // 2, "act")
+        quantize_net(4, ng[4])
+        quantize_net(5, ng[5])
+        for n, acc in accs:
+            add_and_store(n, acc)
+
+        acc3 = second_product(3)
+        acc4 = second_product(4)
+        ng[7] = work.tile([P, C], BF16, name="ng", align_bytes=64, bufs=5)
+        t0 = turn_net(nets[7], 0, "mm", 5)
+        t1 = turn_net(nets[7], 1, "mm", 5)
+        add_and_store(3, acc3)
+        quantize_net(6, ng[6])
+        relu_net(t0, 0, ng[7])
+        relu_net(t1, 1, ng[7], on_vector=True)
+        add_and_store(4, acc4)
+        quantize_net(7, ng[7], 0, 2)
+        quantize_net(7, ng[7], 2, 4)
+        accs = [(n, second_product(n)) for n in (5, 6, 7)]
+        for n, acc in accs:
+            add_and_store(n, acc, parts=2 if n == MT - 1 else 1)

@@ -37,7 +37,6 @@ def tile_material_requirements_planning_s9_kernel(tc, orders, inv_words, inv_sca
         ctx.enter_context(tc.manual_schedule())
 
         ident = keep.tile([P, P], F32, name="ident")
-        dummy = keep.tile([P, 8], F32, name="dummy")
         planes = keep.tile([P, G1, C], U8, name="planes", align_bytes=64)
         inv_sb = [keep.tile([P, G1, 2 * N], U8, name="inv%d" % c, align_bytes=64) for c in range(G2)]
         ord_sb = [keep.tile([P, K1], BF16, name="ord%d" % i, align_bytes=64) for i in range(MT)]
@@ -68,9 +67,7 @@ def tile_material_requirements_planning_s9_kernel(tc, orders, inv_words, inv_sca
             nc.sync.dma_start(out=sh_raw[g][:], in_=shares[g * KP : (g + 1) * KP, :].rearrange("(p j) s -> p j s", j=4))
 
         nc.vector.memset(planes[:].rearrange("p g n -> p (g n)").bitcast(I32), 0)
-        nc.vector.memset(dummy[:], 0.0)
         make_identity(nc, ident[:])
-        nc.scalar.activation(out=dummy[:], in_=dummy[:], func=RELU)
 
         for g in range(G1):
             nc.sync.dma_start(out=ord_sb[0][:, g * KP : (g + 1) * KP], in_=orders[0:P, g * KP : (g + 1) * KP])

@@ -16,6 +16,7 @@ E5M2X4 = mybir.dt.float8_e5m2_x4
 E2M1X4 = mybir.dt.float4_e2m1fn_x4
 SUB = mybir.AluOpType.subtract
 ADD = mybir.AluOpType.add
+MULT = mybir.AluOpType.mult
 RELU = mybir.ActivationFunctionType.Relu
 
 P = 128
@@ -24,8 +25,16 @@ MT = M // P
 G1 = K1 // KP
 G2 = C // KP
 N = 512
-QS_AFTER = {1: 0, 3: 1, 5: 2, 6: 3}
-SI_AFTER = {1: (1, 0), 2: (1, 1), 4: (3, 0), 5: (3, 1)}
+HALF = C // 2
+WN = 256
+NETB = 4
+NGB = 6
+SHB = 1
+QG = {(2, 4): 0, (3, 4): 1, (5, 0): 2, (6, 1): 3}
+QN = {(7, 0): (0,), (7, 1): (1,), (7, 3): (2,)}
+HV = (0, 2, 4, 6, 8, 11, 14)
+QT = {0: (3,), 1: (4,), 2: (5,), 3: (6,), 4: (7,)}
+TT = {1: (7,)}
 
 
 def tile_material_requirements_planning_s9_kernel(tc, orders, inv_words, inv_scales, stock, shares, contract, out):
@@ -33,16 +42,16 @@ def tile_material_requirements_planning_s9_kernel(tc, orders, inv_words, inv_sca
     with ExitStack() as ctx:
         keep = ctx.enter_context(tc.tile_pool(name="keep", bufs=1))
         work = ctx.enter_context(tc.tile_pool(name="work", bufs=3))
-        psum = ctx.enter_context(tc.psum_pool(name="psum", bufs=1))
+        psum = ctx.enter_context(tc.psum_pool(name="psum", bufs=8))
         ctx.enter_context(tc.manual_schedule())
 
         ident = keep.tile([P, P], F32, name="ident")
-        planes = keep.tile([P, G1, C], U8, name="planes", align_bytes=64)
+        planes = [keep.tile([P, G1, HALF], U8, name="planes%d" % h, align_bytes=64) for h in range(2)]
         inv_sb = [keep.tile([P, G1, 2 * N], U8, name="inv%d" % c, align_bytes=64) for c in range(G2)]
         ord_sb = [keep.tile([P, K1], BF16, name="ord%d" % i, align_bytes=64) for i in range(MT)]
         stk_sb = [keep.tile([P, C], BF16, name="stk%d" % i, align_bytes=64) for i in range(MT)]
         sh_raw = [keep.tile([P, 4, S], BF16, name="shr%d" % g, align_bytes=64) for g in range(G2)]
-        sh_grp = [keep.tile([P, S, 4], BF16, name="shg%d" % g, align_bytes=64) for g in range(G2)]
+        sh_grp = {}
         sh_codes = [keep.tile([P, S], U32, name="shc%d" % g, align_bytes=64) for g in range(G2)]
         sh_scales = [keep.tile([P, S], U8, name="shs%d" % g, align_bytes=64) for g in range(G2)]
         ord_codes = [keep.tile([P, G1 * P], U32, name="oc%d" % i, align_bytes=64) for i in range(MT)]
@@ -50,9 +59,33 @@ def tile_material_requirements_planning_s9_kernel(tc, orders, inv_words, inv_sca
         net_codes = [keep.tile([P, G2 * P], U32, name="nc%d" % i, align_bytes=64) for i in range(MT)]
         net_scales = [keep.tile([P, G2 * P], U8, name="ns%d" % i, align_bytes=64) for i in range(MT)]
         con_sb = keep.tile([P, S], BF16, name="con", align_bytes=64)
+        og, nets, ng, srt, warm = {}, {}, {}, {}, []
 
-        def load_orders(i):
-            nc.sync.dma_start(out=ord_sb[i][:], in_=orders[i * P : (i + 1) * P, :])
+        def warm_setup():
+            zero = keep.tile([P, 4 * WN], BF16, name="zero", align_bytes=64)
+            nc.gpsimd.memset(zero[:].bitcast(I32), 0)
+            for j, fmt in enumerate((E4M3X4, E5M2X4)):
+                w = WN if j == 0 else P
+                warm.append((keep.tile([P, w], U32, name="wc%d" % j, align_bytes=64), keep.tile([P, w], U8, name="ws%d" % j, align_bytes=64), fmt, zero))
+
+        def warm_quantize():
+            for codes, scales, fmt, zero in warm:
+                nc.vector.quantize_mx(out=codes[:].bitcast(fmt), scales=scales[:], in_=zero[:, 0 : 4 * codes.shape[1]])
+
+        def warm_passes(acc, n):
+            for j in range(n):
+                nc.tensor.matmul_mx(
+                    out=acc[:, 0:WN],
+                    lhsT=warm[1][0][:].bitcast(E5M2X4),
+                    lhsT_scale=warm[1][1][:],
+                    rhs=warm[0][0][:].bitcast(E4M3X4),
+                    rhs_scale=warm[0][1][:],
+                    start=True,
+                    stop=True,
+                )
+
+        def load_orders(i, c0=0, c1=K1):
+            nc.sync.dma_start(out=ord_sb[i][:, c0:c1], in_=orders[i * P : (i + 1) * P, c0:c1])
 
         def load_stock(i, c0=0, c1=C):
             nc.sync.dma_start(out=stk_sb[i][:, c0:c1], in_=stock[i * P : (i + 1) * P, c0:c1])
@@ -63,222 +96,257 @@ def tile_material_requirements_planning_s9_kernel(tc, orders, inv_words, inv_sca
                 in_=inv_words.rearrange("g p b -> p g b")[:, :, 2 * N * c : 2 * N * (c + 1)].bitcast(I32),
             )
 
+        def load_scales(h):
+            rows = inv_scales.rearrange("g (q r) n -> r q g n", r=4)
+            for r in range(4):
+                nc.sync.dma_start(out=planes[h][r:P:32, :, :].bitcast(I32), in_=rows[r][:, :, h * HALF : (h + 1) * HALF].bitcast(I32))
+
         def load_shares(g):
             nc.sync.dma_start(out=sh_raw[g][:], in_=shares[g * KP : (g + 1) * KP, :].rearrange("(p j) s -> p j s", j=4))
 
-        nc.vector.memset(planes[:].rearrange("p g n -> p (g n)").bitcast(I32), 0)
-        make_identity(nc, ident[:])
-
-        for g in range(G1):
-            nc.sync.dma_start(out=ord_sb[0][:, g * KP : (g + 1) * KP], in_=orders[0:P, g * KP : (g + 1) * KP])
-        for r in range(4):
-            nc.sync.dma_start(
-                out=planes[r:P:32, :, :].bitcast(I32),
-                in_=inv_scales.rearrange("g (q r) n -> r q g n", r=4)[r].bitcast(I32),
-            )
-        load_orders(1)
-        load_inv(0)
-        load_stock(0, 0, C // 2)
-        load_inv(1)
-        load_orders(2)
-        load_stock(1, 0, C // 2)
-        load_inv(2)
-        load_stock(0, C // 2, C)
-        load_inv(3)
-        load_stock(1, C // 2, C)
-        load_shares(0)
-        load_orders(3)
-        load_stock(2)
-        load_shares(1)
-        load_orders(4)
-        load_stock(3)
-        load_shares(2)
-        load_orders(5)
-        load_stock(4)
-        load_shares(3)
-        load_orders(6)
-        load_stock(5)
-        load_orders(7)
-        load_stock(6)
-        load_stock(7)
-        nc.sync.dma_start(out=con_sb[:], in_=contract.partition_broadcast(P))
-
-        def bank(tag, bufs):
-            return psum.tile([P, N], F32, name=tag, tag=tag, bufs=bufs)
+        def bank():
+            return psum.tile([P, N], F32, name="bank")
 
         def turn_orders(i, g, t, slot, width):
             words = ord_sb[i][:].bitcast(F32)
             for u in range(2):
                 nc.tensor.transpose(t[:, u * width + slot * P : u * width + (slot + 1) * P], words[:, 256 * g + u : 256 * (g + 1) : 2], ident[:])
 
-        def orders_half(i, g, tag, bufs, engine_copy, grp):
-            t = bank(tag, bufs)
+        def new_og(i):
+            og[i] = work.tile([P, K1], BF16, name="og", align_bytes=64)
+
+        def orders_half(i, g, engine_copy, t):
             turn_orders(i, g, t, 0, P)
             engine_copy(
-                out=grp[:, g * 512 : (g + 1) * 512].bitcast(F32).rearrange("p (x u) -> p x u", u=2),
+                out=og[i][:, g * 512 : (g + 1) * 512].bitcast(F32).rearrange("p (x u) -> p x u", u=2),
                 in_=t[:, 0:256].rearrange("p (u x) -> p x u", u=2),
             )
 
-        def orders_tile(i, tag, bufs, grp):
-            t = bank(tag, bufs)
+        def orders_tile(i, engine_copy=None, t=None):
+            new_og(i)
+            t = t or bank()
             for g in range(G1):
                 turn_orders(i, g, t, g, 2 * P)
-            nc.scalar.copy(
-                out=grp[:].bitcast(F32).rearrange("p (x u) -> p x u", u=2),
+            (engine_copy or nc.scalar.copy)(
+                out=og[i][:].bitcast(F32).rearrange("p (x u) -> p x u", u=2),
                 in_=t[:].rearrange("p (u x) -> p x u", u=2),
             )
 
-        def quantize_orders(i, grp, a=0, b=G1):
+        def sort_orders(i, engine_copy):
+            srt[i] = work.tile([P, K1 // 2], F32, name="srt", align_bytes=64)
+            engine_copy(
+                out=srt[i][:].rearrange("m (u x) -> m u x", u=2),
+                in_=ord_sb[i][:].bitcast(F32).rearrange("m (x u) -> m u x", u=2),
+            )
+
+        def sorted_tile(i):
+            new_og(i)
+            t = bank()
+            for j in range(4):
+                nc.tensor.transpose(t[:, j * P : (j + 1) * P], srt[i][:, j * P : (j + 1) * P], ident[:])
+            nc.scalar.copy(
+                out=og[i][:].bitcast(F32).rearrange("p (x u) -> p x u", u=2),
+                in_=t[:].rearrange("p (u x) -> p x u", u=2),
+            )
+
+        def quantize_orders(i, a=0, b=G1):
             nc.vector.quantize_mx(
                 out=ord_codes[i][:, a * P : b * P].bitcast(E4M3X4),
                 scales=ord_scales[i][:, a * P : b * P],
-                in_=grp[:, a * 512 : b * 512],
+                in_=og[i][:, a * 512 : b * 512],
             )
 
-        def first_product(i, c):
-            acc = bank("mm", 5)
+        def first_product(i, c, acc=None):
+            acc = acc or bank()
             for g in range(G1):
                 nc.tensor.matmul_mx(
                     out=acc[:],
                     lhsT=ord_codes[i][:, g * P : (g + 1) * P].bitcast(E4M3X4),
                     lhsT_scale=ord_scales[i][:, g * P : (g + 1) * P],
                     rhs=inv_sb[c][:, g, :].bitcast(E2M1X4),
-                    rhs_scale=planes[:, g, c * N : (c + 1) * N],
+                    rhs_scale=planes[c // 2][:, g, (c % 2) * N : (c % 2 + 1) * N],
                     start=(g == 0),
                     stop=(g == G1 - 1),
                 )
             return acc
 
-        def subtract_stock(i, c, acc, net):
+        def new_net(i):
+            nets[i] = work.tile([P, C], BF16, name="net", align_bytes=64, bufs=NETB)
+
+        def subtract_stock(i, c, acc):
             nc.vector.tensor_tensor(
-                out=net[:, c * N : (c + 1) * N].rearrange("m (u p e) -> m u p e", u=2, e=2),
+                out=nets[i][:, c * N : (c + 1) * N].rearrange("m (u p e) -> m u p e", u=2, e=2),
                 in0=acc[:].rearrange("m (p u e) -> m u p e", u=2, e=2),
                 in1=stk_sb[i][:, c * N : (c + 1) * N].rearrange("m (p u e) -> m u p e", u=2, e=2),
                 op=SUB,
             )
 
-        def turn_net(net, h, tag, bufs):
-            t = bank(tag, bufs)
-            words = net[:].bitcast(F32)
+        def gross(i, c):
+            subtract_stock(i, c, first_product(i, c))
+
+        def turn_net(i, h):
+            t = bank()
+            words = nets[i][:].bitcast(F32)
             for cl in range(2):
                 c = 2 * h + cl
                 for u in range(2):
                     nc.tensor.transpose(t[:, u * 256 + cl * P : u * 256 + (cl + 1) * P], words[:, 256 * c + P * u : 256 * c + P * (u + 1)], ident[:])
             return t
 
-        def relu_net(t, h, grp, on_vector=False):
-            o = grp[:, h * 1024 : (h + 1) * 1024].rearrange("p (x u e) -> p x u e", u=2, e=2)
-            i = t[:].bitcast(BF16).rearrange("p (u x e) -> p x u e", u=2, e=2)
+        def relu_net(i, h, t, on_vector=False):
+            if h == 0:
+                ng[i] = work.tile([P, C], BF16, name="ng", align_bytes=64, bufs=NGB)
+            o = ng[i][:, h * 1024 : (h + 1) * 1024].rearrange("p (x u e) -> p x u e", u=2, e=2)
+            src = t[:].bitcast(BF16).rearrange("p (u x e) -> p x u e", u=2, e=2)
             if on_vector:
-                nc.vector.tensor_scalar_max(out=o, in0=i, scalar1=0.0)
+                nc.vector.tensor_scalar_max(out=o, in0=src, scalar1=0.0)
             else:
-                nc.scalar.activation(out=o, in_=i, func=RELU)
+                nc.scalar.activation(out=o, in_=src, func=RELU)
 
-        def quantize_net(i, grp, a=0, b=G2):
+        def net_tile(i):
+            for h in range(2):
+                relu_net(i, h, turn_net(i, h))
+
+        def quantize_net(i, a=0, b=G2):
             nc.vector.quantize_mx(
                 out=net_codes[i][:, a * P : b * P].bitcast(E5M2X4),
                 scales=net_scales[i][:, a * P : b * P],
-                in_=grp[:, a * 512 : b * 512],
+                in_=ng[i][:, a * 512 : b * 512],
             )
 
-        def interleave_shares(g, s0, s1, engine):
+        def new_grp(g):
+            sh_grp[g] = work.tile([P, S, 4], BF16, name="shg", align_bytes=64, bufs=SHB)
+
+        def gpsimd_copy(out, in_):
+            nc.gpsimd.tensor_scalar(out=out, in0=in_, scalar1=1.0, scalar2=0.0, op0=MULT, op1=ADD)
+
+        def interleave_shares(g, s0, s1, engine_copy):
             o = sh_grp[g][:, s0:s1, :].rearrange("p (c i) t -> p c t i", i=4)
             i = sh_raw[g][:, :, s0:s1].rearrange("p t (c i) -> p c t i", i=4)
-            if engine == "act":
-                nc.scalar.copy(out=o, in_=i)
-            else:
-                nc.vector.tensor_copy(out=o, in_=i)
+            engine_copy(out=o, in_=i)
+
+        def interleave_on_gpsimd(g):
+            nc.gpsimd.tensor_scalar(out=sh_grp[g][:], in0=sh_raw[g][:].rearrange("p t s -> p s t"), scalar1=1.0, scalar2=0.0, op0=MULT, op1=ADD)
 
         def quantize_shares(g):
             nc.vector.quantize_mx(out=sh_codes[g][:].bitcast(E4M3X4), scales=sh_scales[g][:], in_=sh_grp[g][:].rearrange("p s t -> p (s t)"))
 
-        def second_product(i):
-            acc = bank("mm", 5)
-            for n, g in enumerate(range(G2)):
+        def second_product(i, s0=0, s1=S):
+            acc = bank()
+            for g in range(G2):
                 nc.tensor.matmul_mx(
-                    out=acc[:],
+                    out=acc[:, 0 : s1 - s0],
                     lhsT=net_codes[i][:, g * P : (g + 1) * P].bitcast(E5M2X4),
                     lhsT_scale=net_scales[i][:, g * P : (g + 1) * P],
-                    rhs=sh_codes[g][:].bitcast(E4M3X4),
-                    rhs_scale=sh_scales[g][:],
-                    start=(n == 0),
-                    stop=(n == G2 - 1),
+                    rhs=sh_codes[g][:, s0:s1].bitcast(E4M3X4),
+                    rhs_scale=sh_scales[g][:, s0:s1],
+                    start=(g == 0),
+                    stop=(g == G2 - 1),
                 )
             return acc
 
-        def add_and_store(i, acc, parts=1):
-            res = work.tile([P, S], F32, name="res", bufs=4)
-            w = S // parts
-            for k in range(parts):
-                nc.vector.tensor_tensor(out=res[:, k * w : (k + 1) * w], in0=acc[:, k * w : (k + 1) * w], in1=con_sb[:, k * w : (k + 1) * w], op=ADD)
-                queue = nc.sync if k % 2 == 0 else nc.scalar
-                queue.dma_start(out=out[i * P : (i + 1) * P, k * w : (k + 1) * w], in_=res[:, k * w : (k + 1) * w])
+        def add_and_store(i, acc, s0=0, s1=S, queue=None):
+            res = work.tile([P, s1 - s0], F32, name="res", bufs=4)
+            nc.vector.tensor_tensor(out=res[:], in0=acc[:, 0 : s1 - s0], in1=con_sb[:, s0:s1], op=ADD)
+            (queue or nc.sync).dma_start(out=out[i * P : (i + 1) * P, s0:s1], in_=res[:])
 
-        og, nets, ng = {}, {}, {}
 
-        def new_og(i):
-            og[i] = work.tile([P, K1], BF16, name="og", align_bytes=64)
-            return og[i]
+        nc.vector.memset(planes[0][:].rearrange("p g n -> p (g n)").bitcast(I32), 0)
+
+        nc.vector.memset(planes[1][:].rearrange("p g n -> p (g n)").bitcast(I32), 0)
+        make_identity(nc, ident[:])
+        load_orders(0)
+        load_orders(1)
+        load_inv(0)
+        load_scales(0)
+        load_inv(1)
+        load_orders(2)
+        load_orders(3)
+        load_scales(1)
+        load_inv(2)
+        load_stock(0, 0, HALF)
+        load_inv(3)
+        load_stock(1, 0, HALF)
+        load_stock(0, HALF, C)
+        load_stock(1, HALF, C)
+        load_orders(4)
+        load_shares(0)
+        load_stock(2)
+        load_orders(5)
+        load_shares(1)
+        load_stock(3)
+        load_orders(6)
+        load_shares(2)
+        load_stock(4)
+        load_orders(7)
+        load_shares(3)
+        load_stock(5)
+        load_stock(6)
+        load_stock(7)
+        nc.sync.dma_start(out=con_sb[:], in_=contract.partition_broadcast(P))
+
+        first = [bank() for j in range(4)]
+        wb = first[3]
 
         new_og(0)
-        orders_half(0, 0, "nt", 2, nc.scalar.copy, og[0])
-        orders_half(0, 1, "nt", 2, nc.vector.tensor_copy, og[0])
-        quantize_orders(0, og[0], 0, 1)
-        quantize_orders(0, og[0], 1, 2)
-        orders_tile(1, "ot", 1, new_og(1))
-        quantize_orders(1, og[1])
+        orders_half(0, 0, nc.scalar.copy, first[0])
+        orders_half(0, 1, nc.vector.tensor_copy, first[1])
+        orders_tile(1, None, first[2])
 
-        for tiles in ((0, 1), (2,), (3,), (4,), (5,), (6,), (7,)):
-            i = tiles[-1]
-            for x in tiles:
-                nets[x] = work.tile([P, C], BF16, name="net", align_bytes=64)
+        quantize_orders(0)
+        quantize_orders(1)
+        new_net(0)
+        new_net(1)
+        a = {(x, c): first_product(x, c, wb if x + c == 0 else None) for x in range(2) for c in range(2)}
+        for i in (2, 3):
+            sort_orders(i, nc.scalar.copy)
+        for i in (2, 3):
+            sorted_tile(i)
+        for c in range(2):
+            subtract_stock(0, c, a[0, c])
+        quantize_orders(2)
+        b = {(x, c): first_product(x, c) for c in range(2, 4) for x in range(2)}
+        for c in range(2):
+            subtract_stock(1, c, a[1, c])
+        quantize_orders(3)
+        sort_orders(4, nc.scalar.copy)
+        for c in range(2, 4):
+            for x in range(2):
+                subtract_stock(x, c, b[x, c])
+
+        def group(g):
+            quantize_orders(g + 4)
+            quantize_shares(g)
+            if g < G2 - 1:
+                new_grp(g + 1)
+                interleave_on_gpsimd(g + 1)
+
+        halves = [(n, h) for n in range(MT) for h in range(2)]
+        new_grp(0)
+        interleave_on_gpsimd(0)
+        for i in range(2, MT):
+            new_net(i)
             for c in range(G2):
-                for x in tiles:
-                    acc = first_product(x, c)
-                    if x == 1 and c == 0:
-                        orders_tile(2, "ot", 1, new_og(2))
-                        interleave_shares(0, 0, S // 2, "act")
-                        interleave_shares(0, S // 2, S, "act")
-                    if c == 2 and x >= 4:
-                        quantize_net(x - 4, ng[x - 4])
-                    subtract_stock(x, c, acc, nets[x])
-                    if x == 1 and c == 1:
-                        quantize_orders(2, og[2])
-                    if c == 0 and 2 <= x < MT - 1:
-                        quantize_orders(x + 1, og[x + 1])
-                if i == 4 and c == 1:
-                    interleave_shares(2, S // 2, S, "dve")
-            if i == 3:
-                interleave_shares(2, 0, S // 2, "dve")
-            if i in QS_AFTER:
-                quantize_shares(QS_AFTER[i])
-            accs = [(n, second_product(n)) for n in (range(3) if i == MT - 1 else ())]
+                gross(i, c)
+                if (i, c) in QG:
+                    group(QG[i, c])
+                for k in QN.get((i, c), ()):
+                    quantize_net(k)
             if i + 2 < MT:
-                orders_tile(i + 2, "ot", 1, new_og(i + 2))
-            ng[i - 1] = work.tile([P, C], BF16, name="ng", align_bytes=64, bufs=5)
-            for h in range(2):
-                t = turn_net(nets[i - 1], h, "nt", 2)
-                relu_net(t, h, ng[i - 1], on_vector=(i == 1 and h == 0))
-            if i in SI_AFTER:
-                g, h = SI_AFTER[i]
-                interleave_shares(g, h * S // 2, (h + 1) * S // 2, "act")
-        quantize_net(4, ng[4])
-        quantize_net(5, ng[5])
-        for n, acc in accs:
-            add_and_store(n, acc)
+                sorted_tile(i + 2)
+            if (i, 4) in QG:
+                group(QG[i, 4])
+            if i + 3 < MT:
+                sort_orders(i + 3, nc.scalar.copy)
+            for n, h in halves[HV[i - 2] : HV[i - 1]]:
+                relu_net(n, h, turn_net(n, h))
 
-        acc3 = second_product(3)
-        acc4 = second_product(4)
-        ng[7] = work.tile([P, C], BF16, name="ng", align_bytes=64, bufs=5)
-        t0 = turn_net(nets[7], 0, "mm", 5)
-        t1 = turn_net(nets[7], 1, "mm", 5)
-        add_and_store(3, acc3)
-        quantize_net(6, ng[6])
-        relu_net(t0, 0, ng[7])
-        relu_net(t1, 1, ng[7], on_vector=True)
-        add_and_store(4, acc4)
-        quantize_net(7, ng[7], 0, 2)
-        quantize_net(7, ng[7], 2, 4)
-        accs = [(n, second_product(n)) for n in (5, 6, 7)]
-        for n, acc in accs:
-            add_and_store(n, acc, parts=2 if n == MT - 1 else 1)
+        for n in range(0, MT - 1):
+            acc = second_product(n)
+            for k in QT.get(n, ()):
+                quantize_net(k)
+            add_and_store(n, acc)
+            for k in TT.get(n, ()):
+                net_tile(k)
+        for s0, s1, q in ((0, 256, nc.sync), (256, 512, nc.scalar)):
+            add_and_store(MT - 1, second_product(MT - 1, s0, s1), s0, s1, q)

@@ -26,13 +26,16 @@ G1 = K1 // KP
 G2 = C // KP
 N = 512
 HALF = C // 2
+OGS = 99
+GS = 512
 WN = 256
-NETB = 4
+NETB = 5
 NGB = 6
 SHB = 1
-QG = {(2, 4): 0, (3, 4): 1, (5, 0): 2, (6, 1): 3}
-QN = {(7, 0): (0,), (7, 1): (1,), (7, 3): (2,)}
-HV = (0, 2, 4, 6, 8, 11, 14)
+QG = {(2, 4): 0, (4, 1): 1, (5, 3): 2, (7, 1): 3}
+QN = {(7, 3): (2,)}
+QNG = {2: (0,), 3: (1,)}
+HV = (0, 1, 2, 5, 8, 11, 14)
 QT = {0: (3,), 1: (4,), 2: (5,), 3: (6,), 4: (7,)}
 TT = {1: (7,)}
 
@@ -113,7 +116,10 @@ def tile_material_requirements_planning_s9_kernel(tc, orders, inv_words, inv_sca
                 nc.tensor.transpose(t[:, u * width + slot * P : u * width + (slot + 1) * P], words[:, 256 * g + u : 256 * (g + 1) : 2], ident[:])
 
         def new_og(i):
-            og[i] = work.tile([P, K1], BF16, name="og", align_bytes=64)
+            if i == OGS:
+                og[i] = work.tile([P, K1], BF16, name="shg", align_bytes=64, bufs=SHB)
+            else:
+                og[i] = work.tile([P, K1], BF16, name="og", align_bytes=64)
 
         def orders_half(i, g, engine_copy, t):
             turn_orders(i, g, t, 0, P)
@@ -226,14 +232,14 @@ def tile_material_requirements_planning_s9_kernel(tc, orders, inv_words, inv_sca
             engine_copy(out=o, in_=i)
 
         def interleave_on_gpsimd(g):
-            nc.gpsimd.tensor_scalar(out=sh_grp[g][:], in0=sh_raw[g][:].rearrange("p t s -> p s t"), scalar1=1.0, scalar2=0.0, op0=MULT, op1=ADD)
+            nc.gpsimd.tensor_scalar(out=sh_grp[g][:, 0:GS, :], in0=sh_raw[g][:, :, 0:GS].rearrange("p t s -> p s t"), scalar1=1.0, scalar2=0.0, op0=MULT, op1=ADD)
 
         def quantize_shares(g):
             nc.vector.quantize_mx(out=sh_codes[g][:].bitcast(E4M3X4), scales=sh_scales[g][:], in_=sh_grp[g][:].rearrange("p s t -> p (s t)"))
 
-        def second_product(i, s0=0, s1=S):
-            acc = bank()
-            for g in range(G2):
+        def second_product(i, s0=0, s1=S, acc=None, groups=range(G2)):
+            acc = acc or bank()
+            for g in groups:
                 nc.tensor.matmul_mx(
                     out=acc[:, 0 : s1 - s0],
                     lhsT=net_codes[i][:, g * P : (g + 1) * P].bitcast(E5M2X4),
@@ -246,14 +252,13 @@ def tile_material_requirements_planning_s9_kernel(tc, orders, inv_words, inv_sca
             return acc
 
         def add_and_store(i, acc, s0=0, s1=S, queue=None):
-            res = work.tile([P, s1 - s0], F32, name="res", bufs=4)
+            res = work.tile([P, s1 - s0], F32, name="res", bufs=MT + 3)
             nc.vector.tensor_tensor(out=res[:], in0=acc[:, 0 : s1 - s0], in1=con_sb[:, s0:s1], op=ADD)
             (queue or nc.sync).dma_start(out=out[i * P : (i + 1) * P, s0:s1], in_=res[:])
 
 
-        nc.vector.memset(planes[0][:].rearrange("p g n -> p (g n)").bitcast(I32), 0)
-
-        nc.vector.memset(planes[1][:].rearrange("p g n -> p (g n)").bitcast(I32), 0)
+        for h in range(2):
+            nc.vector.memset(planes[h][:].rearrange("p g n -> p (g n)").bitcast(I32), 0)
         make_identity(nc, ident[:])
         load_orders(0)
         load_orders(1)
@@ -270,17 +275,17 @@ def tile_material_requirements_planning_s9_kernel(tc, orders, inv_words, inv_sca
         load_stock(0, HALF, C)
         load_stock(1, HALF, C)
         load_orders(4)
+        load_orders(5)
         load_shares(0)
         load_stock(2)
-        load_orders(5)
-        load_shares(1)
-        load_stock(3)
         load_orders(6)
-        load_shares(2)
-        load_stock(4)
         load_orders(7)
-        load_shares(3)
+        load_stock(3)
+        load_shares(1)
+        load_stock(4)
+        load_shares(2)
         load_stock(5)
+        load_shares(3)
         load_stock(6)
         load_stock(7)
         nc.sync.dma_start(out=con_sb[:], in_=contract.partition_broadcast(P))
@@ -309,13 +314,18 @@ def tile_material_requirements_planning_s9_kernel(tc, orders, inv_words, inv_sca
         for c in range(2):
             subtract_stock(1, c, a[1, c])
         quantize_orders(3)
-        sort_orders(4, nc.scalar.copy)
+        for i in (4, 5):
+            sort_orders(i, nc.scalar.copy)
         for c in range(2, 4):
             for x in range(2):
                 subtract_stock(x, c, b[x, c])
 
         def group(g):
-            quantize_orders(g + 4)
+            for i in (2 * g + 4, 2 * g + 5):
+                if i < MT:
+                    quantize_orders(i)
+            for k in QNG.get(g, ()):
+                quantize_net(k)
             quantize_shares(g)
             if g < G2 - 1:
                 new_grp(g + 1)
@@ -332,21 +342,23 @@ def tile_material_requirements_planning_s9_kernel(tc, orders, inv_words, inv_sca
                     group(QG[i, c])
                 for k in QN.get((i, c), ()):
                     quantize_net(k)
-            if i + 2 < MT:
-                sorted_tile(i + 2)
+            if i < 4:
+                for j in (2 * i, 2 * i + 1):
+                    sorted_tile(j)
             if (i, 4) in QG:
                 group(QG[i, 4])
-            if i + 3 < MT:
-                sort_orders(i + 3, nc.scalar.copy)
+            if i == 2:
+                for j in (6, 7):
+                    sort_orders(j, nc.scalar.copy)
             for n, h in halves[HV[i - 2] : HV[i - 1]]:
                 relu_net(n, h, turn_net(n, h))
 
-        for n in range(0, MT - 1):
+        for n in range(0, MT - 2):
             acc = second_product(n)
             for k in QT.get(n, ()):
                 quantize_net(k)
             add_and_store(n, acc)
             for k in TT.get(n, ()):
                 net_tile(k)
-        for s0, s1, q in ((0, 256, nc.sync), (256, 512, nc.scalar)):
-            add_and_store(MT - 1, second_product(MT - 1, s0, s1), s0, s1, q)
+        for n, s0, s1, q in ((6, 0, 256, nc.sync), (6, 256, 512, nc.sync), (7, 0, 256, nc.sync), (7, 256, 384, nc.scalar), (7, 384, 512, nc.sync)):
+            add_and_store(n, second_product(n, s0, s1), s0, s1, q)

@@ -26,6 +26,8 @@ G1 = K1 // KP
 G2 = C // KP
 N = 512
 HALF = C // 2
+PIECES = ((0, 2), (2, 4))
+IPIECES = ((0, 1), (1, 2), (2, 3), (3, 4))
 OGS = 99
 GS = 512
 WN = 256
@@ -49,8 +51,8 @@ def tile_material_requirements_planning_s9_kernel(tc, orders, inv_words, inv_sca
         ctx.enter_context(tc.manual_schedule())
 
         ident = keep.tile([P, P], F32, name="ident")
-        planes = [keep.tile([P, G1, HALF], U8, name="planes%d" % h, align_bytes=64) for h in range(2)]
-        inv_sb = [keep.tile([P, G1, 2 * N], U8, name="inv%d" % c, align_bytes=64) for c in range(G2)]
+        planes = [keep.tile([P, G1, (b - a) * N], U8, name="planes%d" % a, align_bytes=64) for a, b in PIECES]
+        inv_sb = [keep.tile([P, G1, 2 * N * (b - a)], U8, name="inv%d" % a, align_bytes=64) for a, b in IPIECES]
         ord_sb = [keep.tile([P, K1], BF16, name="ord%d" % i, align_bytes=64) for i in range(MT)]
         stk_sb = [keep.tile([P, C], BF16, name="stk%d" % i, align_bytes=64) for i in range(MT)]
         sh_raw = [keep.tile([P, 4, S], BF16, name="shr%d" % g, align_bytes=64) for g in range(G2)]
@@ -66,7 +68,7 @@ def tile_material_requirements_planning_s9_kernel(tc, orders, inv_words, inv_sca
 
         def warm_setup():
             zero = keep.tile([P, 4 * WN], BF16, name="zero", align_bytes=64)
-            nc.gpsimd.memset(zero[:].bitcast(I32), 0)
+            nc.vector.memset(zero[:].bitcast(I32), 0)
             for j, fmt in enumerate((E4M3X4, E5M2X4)):
                 w = WN if j == 0 else P
                 warm.append((keep.tile([P, w], U32, name="wc%d" % j, align_bytes=64), keep.tile([P, w], U8, name="ws%d" % j, align_bytes=64), fmt, zero))
@@ -96,13 +98,13 @@ def tile_material_requirements_planning_s9_kernel(tc, orders, inv_words, inv_sca
         def load_inv(c):
             nc.sync.dma_start(
                 out=inv_sb[c][:].bitcast(I32),
-                in_=inv_words.rearrange("g p b -> p g b")[:, :, 2 * N * c : 2 * N * (c + 1)].bitcast(I32),
+                in_=inv_words.rearrange("g p b -> p g b")[:, :, 2 * N * IPIECES[c][0] : 2 * N * IPIECES[c][1]].bitcast(I32),
             )
 
         def load_scales(h):
             rows = inv_scales.rearrange("g (q r) n -> r q g n", r=4)
             for r in range(4):
-                nc.sync.dma_start(out=planes[h][r:P:32, :, :].bitcast(I32), in_=rows[r][:, :, h * HALF : (h + 1) * HALF].bitcast(I32))
+                nc.sync.dma_start(out=planes[h][r:P:32, :, :].bitcast(I32), in_=rows[r][:, :, PIECES[h][0] * N : PIECES[h][1] * N].bitcast(I32))
 
         def load_shares(g):
             nc.sync.dma_start(out=sh_raw[g][:], in_=shares[g * KP : (g + 1) * KP, :].rearrange("(p j) s -> p j s", j=4))
@@ -119,7 +121,7 @@ def tile_material_requirements_planning_s9_kernel(tc, orders, inv_words, inv_sca
             if i == OGS:
                 og[i] = work.tile([P, K1], BF16, name="shg", align_bytes=64, bufs=SHB)
             else:
-                og[i] = work.tile([P, K1], BF16, name="og", align_bytes=64)
+                og[i] = work.tile([P, K1], BF16, name="og", align_bytes=64, bufs=4)
 
         def orders_half(i, g, engine_copy, t):
             turn_orders(i, g, t, 0, P)
@@ -139,7 +141,7 @@ def tile_material_requirements_planning_s9_kernel(tc, orders, inv_words, inv_sca
             )
 
         def sort_orders(i, engine_copy):
-            srt[i] = work.tile([P, K1 // 2], F32, name="srt", align_bytes=64)
+            srt[i] = work.tile([P, K1 // 2], F32, name="srt", align_bytes=64, bufs=4)
             engine_copy(
                 out=srt[i][:].rearrange("m (u x) -> m u x", u=2),
                 in_=ord_sb[i][:].bitcast(F32).rearrange("m (x u) -> m u x", u=2),
@@ -163,14 +165,16 @@ def tile_material_requirements_planning_s9_kernel(tc, orders, inv_words, inv_sca
             )
 
         def first_product(i, c, acc=None):
+            h = [j for j, (a, b) in enumerate(PIECES) if a <= c < b][0]
+            v = [j for j, (a, b) in enumerate(IPIECES) if a <= c < b][0]
             acc = acc or bank()
             for g in range(G1):
                 nc.tensor.matmul_mx(
                     out=acc[:],
                     lhsT=ord_codes[i][:, g * P : (g + 1) * P].bitcast(E4M3X4),
                     lhsT_scale=ord_scales[i][:, g * P : (g + 1) * P],
-                    rhs=inv_sb[c][:, g, :].bitcast(E2M1X4),
-                    rhs_scale=planes[c // 2][:, g, (c % 2) * N : (c % 2 + 1) * N],
+                    rhs=inv_sb[v][:, g, 2 * N * (c - IPIECES[v][0]) : 2 * N * (c - IPIECES[v][0] + 1)].bitcast(E2M1X4),
+                    rhs_scale=planes[h][:, g, (c - PIECES[h][0]) * N : (c - PIECES[h][0] + 1) * N],
                     start=(g == 0),
                     stop=(g == G1 - 1),
                 )
@@ -257,10 +261,13 @@ def tile_material_requirements_planning_s9_kernel(tc, orders, inv_words, inv_sca
             (queue or nc.sync).dma_start(out=out[i * P : (i + 1) * P, s0:s1], in_=res[:])
 
 
-        for h in range(2):
-            nc.vector.memset(planes[h][:].rearrange("p g n -> p (g n)").bitcast(I32), 0)
+        nc.vector.memset(planes[0][:].rearrange("p g n -> p (g n)").bitcast(I32), 0)
+
+        for plane in planes[1:]:
+            nc.vector.memset(plane[:].rearrange("p g n -> p (g n)").bitcast(I32), 0)
         make_identity(nc, ident[:])
-        load_orders(0)
+        load_orders(0, 0, KP)
+        load_orders(0, KP, K1)
         load_orders(1)
         load_inv(0)
         load_scales(0)
@@ -298,7 +305,8 @@ def tile_material_requirements_planning_s9_kernel(tc, orders, inv_words, inv_sca
         orders_half(0, 1, nc.vector.tensor_copy, first[1])
         orders_tile(1, None, first[2])
 
-        quantize_orders(0)
+        quantize_orders(0, 0, 1)
+        quantize_orders(0, 1, 2)
         quantize_orders(1)
         new_net(0)
         new_net(1)

@@ -50,19 +50,25 @@ def tile_material_requirements_planning_s9_kernel(tc, orders, inv_words, inv_sca
         psum = ctx.enter_context(tc.psum_pool(name="psum", bufs=8))
         ctx.enter_context(tc.manual_schedule())
 
+        def placed(shape, dtype, size, name, start):
+            n = shape[1] * (shape[2] if len(shape) == 3 else 1)
+            whole = keep.tile([P, n + 256 // size], dtype, name=name, align_bytes=256)
+            flat = whole[:, start // size : start // size + n]
+            return flat.rearrange("p (g n) -> p g n", g=shape[1]) if len(shape) == 3 else flat
+
         ident = keep.tile([P, P], F32, name="ident")
-        planes = [keep.tile([P, G1, (b - a) * N], U8, name="planes%d" % a, align_bytes=64) for a, b in PIECES]
-        inv_sb = [keep.tile([P, G1, 2 * N * (b - a)], U8, name="inv%d" % a, align_bytes=64) for a, b in IPIECES]
+        planes = [placed([P, G1, (b - a) * N], U8, 1, "planes%d" % a, 128) for a, b in PIECES]
+        inv_sb = [placed([P, G1, 2 * N * (b - a)], U8, 1, "inv%d" % a, 0) for a, b in IPIECES]
         ord_sb = [keep.tile([P, K1], BF16, name="ord%d" % i, align_bytes=64) for i in range(MT)]
         stk_sb = [keep.tile([P, C], BF16, name="stk%d" % i, align_bytes=64) for i in range(MT)]
         sh_raw = [keep.tile([P, 4, S], BF16, name="shr%d" % g, align_bytes=64) for g in range(G2)]
         sh_grp = {}
-        sh_codes = [keep.tile([P, S], U32, name="shc%d" % g, align_bytes=64) for g in range(G2)]
-        sh_scales = [keep.tile([P, S], U8, name="shs%d" % g, align_bytes=64) for g in range(G2)]
-        ord_codes = [keep.tile([P, G1 * P], U32, name="oc%d" % i, align_bytes=64) for i in range(MT)]
-        ord_scales = [keep.tile([P, G1 * P], U8, name="os%d" % i, align_bytes=64) for i in range(MT)]
-        net_codes = [keep.tile([P, G2 * P], U32, name="nc%d" % i, align_bytes=64) for i in range(MT)]
-        net_scales = [keep.tile([P, G2 * P], U8, name="ns%d" % i, align_bytes=64) for i in range(MT)]
+        sh_codes = [placed([P, S], U32, 4, "shc%d" % g, 0) for g in range(G2)]
+        sh_scales = [placed([P, S], U8, 1, "shs%d" % g, 128) for g in range(G2)]
+        ord_codes = [placed([P, G1 * P], U32, 4, "oc%d" % i, 64) for i in range(MT)]
+        ord_scales = [placed([P, G1 * P], U8, 1, "os%d" % i, 192) for i in range(MT)]
+        net_codes = [placed([P, G2 * P], U32, 4, "nc%d" % i, 64) for i in range(MT)]
+        net_scales = [placed([P, G2 * P], U8, 1, "ns%d" % i, 192) for i in range(MT)]
         con_sb = keep.tile([P, S], BF16, name="con", align_bytes=64)
         og, nets, ng, srt, warm = {}, {}, {}, {}, []
 

@@ -66,9 +66,9 @@ def tile_material_requirements_planning_s9_kernel(tc, orders, inv_words, inv_sca
         sh_codes = [placed([P, S], U32, 4, "shc%d" % g, 0) for g in range(G2)]
         sh_scales = [placed([P, S], U8, 1, "shs%d" % g, 128) for g in range(G2)]
         ord_codes = [placed([P, G1 * P], U32, 4, "oc%d" % i, 64) for i in range(MT)]
-        ord_scales = [placed([P, G1 * P], U8, 1, "os%d" % i, 192) for i in range(MT)]
+        ord_scales = [placed([P, G1 * P], U8, 1, "os%d" % i, 128) for i in range(MT)]
         net_codes = [placed([P, G2 * P], U32, 4, "nc%d" % i, 64) for i in range(MT)]
-        net_scales = [placed([P, G2 * P], U8, 1, "ns%d" % i, 192) for i in range(MT)]
+        net_scales = [placed([P, G2 * P], U8, 1, "ns%d" % i, 128) for i in range(MT)]
         con_sb = keep.tile([P, S], BF16, name="con", align_bytes=64)
         og, nets, ng, srt, warm = {}, {}, {}, {}, []
 

@@ -26,20 +26,27 @@ G1 = K1 // KP
 G2 = C // KP
 N = 512
 HALF = C // 2
-PIECES = ((0, 2), (2, 4))
-IPIECES = ((0, 1), (1, 2), (2, 3), (3, 4))
-OGS = 99
-GS = 512
-WN = 256
-NETB = 5
-NGB = 6
-SHB = 1
-QG = {(2, 4): 0, (4, 1): 1, (5, 3): 2, (7, 1): 3}
-QN = {(7, 3): (2,)}
-QNG = {2: (0,), 3: (1,)}
-HV = (0, 1, 2, 5, 8, 11, 14)
-QT = {0: (3,), 1: (4,), 2: (5,), 3: (6,), 4: (7,)}
-TT = {1: (7,)}
+PIECES = ((0, 1), (1, 2), (2, 4))
+NETB = 8
+NGB = 16
+RESB = 9
+WN = 512
+WARM1 = 0
+WARM2 = 0
+HEAD = 4
+BYPASS = 1
+GATE_TILE = 7
+LOADS = 'o0 o1 o2 o3 i0 c0 o4 o5 i1 c1 a0 a1 a2 a3 o6 o7 a4 a5 s0 i2 c2 a6 i3 a7 s1 b0 s2 b1 b2 b3 s3 b4 b5 b6 b7'
+HALVES = "a0 a1 a2 a3 b0 a4 a5 a6 a7 b1 b2 b3 b4 b5 b6 b7"
+LAG = 1
+RUNS = {4: ((4, 5), 0), 10: ((6, 7), 4), 22: ((), 5)}
+SORT_AFTER = {0: (4, 5), 4: (6, 7)}
+AFTER_RUN = {10: 'x1'}
+AFTER_SUB = {3: 'o4', 4: 'o5', 10: 'o6 o7 g0', 16: 'a0 w0 g2', 22: 'a1 w1 w2 g3', 28: 'b0 w3'}
+QT = {1: 'b2 a4', 2: 'b3 a5', 3: 'b4 a6', 4: 'b5 a7', 5: 'b6', 6: 'b7'}
+AFTER_LAST = 'a2 b1 a3'
+LAST_RUN = 0
+HOLD = 2
 
 
 def tile_material_requirements_planning_s9_kernel(tc, orders, inv_words, inv_scales, stock, shares, contract, out):
@@ -47,7 +54,7 @@ def tile_material_requirements_planning_s9_kernel(tc, orders, inv_words, inv_sca
     with ExitStack() as ctx:
         keep = ctx.enter_context(tc.tile_pool(name="keep", bufs=1))
         work = ctx.enter_context(tc.tile_pool(name="work", bufs=3))
-        psum = ctx.enter_context(tc.psum_pool(name="psum", bufs=8))
+        psum = ctx.enter_context(tc.psum_pool(name="psum", bufs=1))
         ctx.enter_context(tc.manual_schedule())
 
         def placed(shape, dtype, size, name, start):
@@ -58,11 +65,10 @@ def tile_material_requirements_planning_s9_kernel(tc, orders, inv_words, inv_sca
 
         ident = keep.tile([P, P], F32, name="ident")
         planes = [placed([P, G1, (b - a) * N], U8, 1, "planes%d" % a, 128) for a, b in PIECES]
-        inv_sb = [placed([P, G1, 2 * N * (b - a)], U8, 1, "inv%d" % a, 0) for a, b in IPIECES]
+        inv_sb = [placed([P, G1, 2 * N], U8, 1, "inv%d" % c, 0) for c in range(G2)]
         ord_sb = [keep.tile([P, K1], BF16, name="ord%d" % i, align_bytes=64) for i in range(MT)]
         stk_sb = [keep.tile([P, C], BF16, name="stk%d" % i, align_bytes=64) for i in range(MT)]
         sh_raw = [keep.tile([P, 4, S], BF16, name="shr%d" % g, align_bytes=64) for g in range(G2)]
-        sh_grp = {}
         sh_codes = [placed([P, S], U32, 4, "shc%d" % g, 0) for g in range(G2)]
         sh_scales = [placed([P, S], U8, 1, "shs%d" % g, 128) for g in range(G2)]
         ord_codes = [placed([P, G1 * P], U32, 4, "oc%d" % i, 64) for i in range(MT)]
@@ -70,30 +76,7 @@ def tile_material_requirements_planning_s9_kernel(tc, orders, inv_words, inv_sca
         net_codes = [placed([P, G2 * P], U32, 4, "nc%d" % i, 64) for i in range(MT)]
         net_scales = [placed([P, G2 * P], U8, 1, "ns%d" % i, 128) for i in range(MT)]
         con_sb = keep.tile([P, S], BF16, name="con", align_bytes=64)
-        og, nets, ng, srt, warm = {}, {}, {}, {}, []
-
-        def warm_setup():
-            zero = keep.tile([P, 4 * WN], BF16, name="zero", align_bytes=64)
-            nc.vector.memset(zero[:].bitcast(I32), 0)
-            for j, fmt in enumerate((E4M3X4, E5M2X4)):
-                w = WN if j == 0 else P
-                warm.append((keep.tile([P, w], U32, name="wc%d" % j, align_bytes=64), keep.tile([P, w], U8, name="ws%d" % j, align_bytes=64), fmt, zero))
-
-        def warm_quantize():
-            for codes, scales, fmt, zero in warm:
-                nc.vector.quantize_mx(out=codes[:].bitcast(fmt), scales=scales[:], in_=zero[:, 0 : 4 * codes.shape[1]])
-
-        def warm_passes(acc, n):
-            for j in range(n):
-                nc.tensor.matmul_mx(
-                    out=acc[:, 0:WN],
-                    lhsT=warm[1][0][:].bitcast(E5M2X4),
-                    lhsT_scale=warm[1][1][:],
-                    rhs=warm[0][0][:].bitcast(E4M3X4),
-                    rhs_scale=warm[0][1][:],
-                    start=True,
-                    stop=True,
-                )
+        sh_grp, og, nets, ng, srt, acc1 = {}, {}, {}, {}, {}, {}
 
         def load_orders(i, c0=0, c1=K1):
             nc.sync.dma_start(out=ord_sb[i][:, c0:c1], in_=orders[i * P : (i + 1) * P, c0:c1])
@@ -104,7 +87,7 @@ def tile_material_requirements_planning_s9_kernel(tc, orders, inv_words, inv_sca
         def load_inv(c):
             nc.sync.dma_start(
                 out=inv_sb[c][:].bitcast(I32),
-                in_=inv_words.rearrange("g p b -> p g b")[:, :, 2 * N * IPIECES[c][0] : 2 * N * IPIECES[c][1]].bitcast(I32),
+                in_=inv_words.rearrange("g p b -> p g b")[:, :, 2 * N * c : 2 * N * (c + 1)].bitcast(I32),
             )
 
         def load_scales(h):
@@ -115,36 +98,50 @@ def tile_material_requirements_planning_s9_kernel(tc, orders, inv_words, inv_sca
         def load_shares(g):
             nc.sync.dma_start(out=sh_raw[g][:], in_=shares[g * KP : (g + 1) * KP, :].rearrange("(p j) s -> p j s", j=4))
 
-        def bank():
-            return psum.tile([P, N], F32, name="bank")
+        ring, held = list(range(8)), []
 
-        def turn_orders(i, g, t, slot, width):
+        def bank(slow=False):
+            b = ring.pop(0)
+            if slow:
+                held.append([b, HOLD * len(held)])
+            else:
+                ring.append(b)
+                for x in held:
+                    x[1] = x[1] - 1
+            return psum.tile([P, N], F32, name="bank%d" % b)
+
+        def release():
+            while held and held[0][1] <= 0:
+                ring.append(held.pop(0)[0])
+
+        def new_og(i):
+            if i == GATE_TILE:
+                og[i] = work.tile([P, K1], BF16, name="shg", align_bytes=64, bufs=1)
+            else:
+                og[i] = work.tile([P, K1], BF16, name="og", align_bytes=64, bufs=4)
+
+        def copy_words(engine_copy, dst, t, width):
+            engine_copy(
+                out=dst.bitcast(F32).rearrange("p (x u) -> p x u", u=2),
+                in_=t[:, 0 : 2 * width].rearrange("p (u x) -> p x u", u=2),
+            )
+
+        def turn_unsorted(i, g, t, slot, width):
             words = ord_sb[i][:].bitcast(F32)
             for u in range(2):
                 nc.tensor.transpose(t[:, u * width + slot * P : u * width + (slot + 1) * P], words[:, 256 * g + u : 256 * (g + 1) : 2], ident[:])
 
-        def new_og(i):
-            if i == OGS:
-                og[i] = work.tile([P, K1], BF16, name="shg", align_bytes=64, bufs=SHB)
-            else:
-                og[i] = work.tile([P, K1], BF16, name="og", align_bytes=64, bufs=4)
+        def orders_half(i, g, engine_copy):
+            t = bank()
+            turn_unsorted(i, g, t, 0, P)
+            copy_words(engine_copy, og[i][:, g * KP : (g + 1) * KP], t, P)
 
-        def orders_half(i, g, engine_copy, t):
-            turn_orders(i, g, t, 0, P)
-            engine_copy(
-                out=og[i][:, g * 512 : (g + 1) * 512].bitcast(F32).rearrange("p (x u) -> p x u", u=2),
-                in_=t[:, 0:256].rearrange("p (u x) -> p x u", u=2),
-            )
-
-        def orders_tile(i, engine_copy=None, t=None):
+        def orders_whole(i, engine_copy):
             new_og(i)
-            t = t or bank()
+            t = bank()
             for g in range(G1):
-                turn_orders(i, g, t, g, 2 * P)
-            (engine_copy or nc.scalar.copy)(
-                out=og[i][:].bitcast(F32).rearrange("p (x u) -> p x u", u=2),
-                in_=t[:].rearrange("p (u x) -> p x u", u=2),
-            )
+                turn_unsorted(i, g, t, g, 2 * P)
+            copy_words(engine_copy, og[i][:], t, 2 * P)
 
         def sort_orders(i, engine_copy):
             srt[i] = work.tile([P, K1 // 2], F32, name="srt", align_bytes=64, bufs=4)
@@ -153,103 +150,95 @@ def tile_material_requirements_planning_s9_kernel(tc, orders, inv_words, inv_sca
                 in_=ord_sb[i][:].bitcast(F32).rearrange("m (x u) -> m u x", u=2),
             )
 
-        def sorted_tile(i):
+        def turn_sorted(i, engine_copy=nc.scalar.copy):
             new_og(i)
             t = bank()
             for j in range(4):
                 nc.tensor.transpose(t[:, j * P : (j + 1) * P], srt[i][:, j * P : (j + 1) * P], ident[:])
-            nc.scalar.copy(
-                out=og[i][:].bitcast(F32).rearrange("p (x u) -> p x u", u=2),
-                in_=t[:].rearrange("p (u x) -> p x u", u=2),
-            )
+            copy_words(engine_copy, og[i][:], t, 2 * P)
+
+        def turn_sorted_by_pass(i):
+            new_og(i)
+            t = bank()
+            for j in range(4):
+                nc.tensor.transpose(t[:, j * P : (j + 1) * P], srt[i][:, j * P : (j + 1) * P], ident[:])
+            for g in range(G1):
+                nc.scalar.copy(
+                    out=og[i][:, g * KP : (g + 1) * KP].bitcast(F32).rearrange("p (m u) -> p m u", u=2),
+                    in_=t[:].rearrange("p (u g m) -> p g m u", u=2, g=G1)[:, g],
+                )
 
         def quantize_orders(i, a=0, b=G1):
             nc.vector.quantize_mx(
                 out=ord_codes[i][:, a * P : b * P].bitcast(E4M3X4),
                 scales=ord_scales[i][:, a * P : b * P],
-                in_=og[i][:, a * 512 : b * 512],
+                in_=og[i][:, a * KP : b * KP],
             )
 
-        def first_product(i, c, acc=None):
+        def first_product(i, c):
             h = [j for j, (a, b) in enumerate(PIECES) if a <= c < b][0]
-            v = [j for j, (a, b) in enumerate(IPIECES) if a <= c < b][0]
-            acc = acc or bank()
+            release()
+            acc1[i, c] = bank()
             for g in range(G1):
                 nc.tensor.matmul_mx(
-                    out=acc[:],
+                    out=acc1[i, c][:],
                     lhsT=ord_codes[i][:, g * P : (g + 1) * P].bitcast(E4M3X4),
                     lhsT_scale=ord_scales[i][:, g * P : (g + 1) * P],
-                    rhs=inv_sb[v][:, g, 2 * N * (c - IPIECES[v][0]) : 2 * N * (c - IPIECES[v][0] + 1)].bitcast(E2M1X4),
+                    rhs=inv_sb[c][:, g, :].bitcast(E2M1X4),
                     rhs_scale=planes[h][:, g, (c - PIECES[h][0]) * N : (c - PIECES[h][0] + 1) * N],
                     start=(g == 0),
                     stop=(g == G1 - 1),
                 )
-            return acc
 
-        def new_net(i):
-            nets[i] = work.tile([P, C], BF16, name="net", align_bytes=64, bufs=NETB)
-
-        def subtract_stock(i, c, acc):
+        def subtract_stock(i, c):
+            if c % 2 == 0:
+                nets[i, c // 2] = work.tile([P, HALF], BF16, name="net", align_bytes=64, bufs=NETB)
             nc.vector.tensor_tensor(
-                out=nets[i][:, c * N : (c + 1) * N].rearrange("m (u p e) -> m u p e", u=2, e=2),
-                in0=acc[:].rearrange("m (p u e) -> m u p e", u=2, e=2),
+                out=nets[i, c // 2][:, c % 2 * N : (c % 2 + 1) * N].rearrange("m (u p e) -> m u p e", u=2, e=2),
+                in0=acc1[i, c][:].rearrange("m (p u e) -> m u p e", u=2, e=2),
                 in1=stk_sb[i][:, c * N : (c + 1) * N].rearrange("m (p u e) -> m u p e", u=2, e=2),
                 op=SUB,
             )
 
-        def gross(i, c):
-            subtract_stock(i, c, first_product(i, c))
-
-        def turn_net(i, h):
-            t = bank()
-            words = nets[i][:].bitcast(F32)
+        def turn_net(i, h, on_vector=False):
+            t = bank(True)
+            words = nets[i, h][:].bitcast(F32)
             for cl in range(2):
-                c = 2 * h + cl
                 for u in range(2):
-                    nc.tensor.transpose(t[:, u * 256 + cl * P : u * 256 + (cl + 1) * P], words[:, 256 * c + P * u : 256 * c + P * (u + 1)], ident[:])
-            return t
-
-        def relu_net(i, h, t, on_vector=False):
-            if h == 0:
-                ng[i] = work.tile([P, C], BF16, name="ng", align_bytes=64, bufs=NGB)
-            o = ng[i][:, h * 1024 : (h + 1) * 1024].rearrange("p (x u e) -> p x u e", u=2, e=2)
+                    nc.tensor.transpose(t[:, u * 256 + cl * P : u * 256 + (cl + 1) * P], words[:, 256 * cl + P * u : 256 * cl + P * (u + 1)], ident[:])
+            ng[i, h] = work.tile([P, HALF], BF16, name="ng", align_bytes=64, bufs=NGB)
+            o = ng[i, h][:].rearrange("p (x u e) -> p x u e", u=2, e=2)
             src = t[:].bitcast(BF16).rearrange("p (u x e) -> p x u e", u=2, e=2)
             if on_vector:
                 nc.vector.tensor_scalar_max(out=o, in0=src, scalar1=0.0)
             else:
                 nc.scalar.activation(out=o, in_=src, func=RELU)
 
-        def net_tile(i):
-            for h in range(2):
-                relu_net(i, h, turn_net(i, h))
-
-        def quantize_net(i, a=0, b=G2):
+        def quantize_net(i, h):
             nc.vector.quantize_mx(
-                out=net_codes[i][:, a * P : b * P].bitcast(E5M2X4),
-                scales=net_scales[i][:, a * P : b * P],
-                in_=ng[i][:, a * 512 : b * 512],
+                out=net_codes[i][:, 2 * h * P : 2 * (h + 1) * P].bitcast(E5M2X4),
+                scales=net_scales[i][:, 2 * h * P : 2 * (h + 1) * P],
+                in_=ng[i, h][:],
             )
 
-        def new_grp(g):
-            sh_grp[g] = work.tile([P, S, 4], BF16, name="shg", align_bytes=64, bufs=SHB)
+        def interleave_on_scalar(g):
+            sh_grp[g] = work.tile([P, S, 4], BF16, name="shx", align_bytes=64, bufs=1)
+            nc.scalar.copy(
+                out=sh_grp[g][:].rearrange("p (c i) t -> p c t i", i=4),
+                in_=sh_raw[g][:].rearrange("p t (c i) -> p c t i", i=4),
+            )
 
-        def gpsimd_copy(out, in_):
-            nc.gpsimd.tensor_scalar(out=out, in0=in_, scalar1=1.0, scalar2=0.0, op0=MULT, op1=ADD)
-
-        def interleave_shares(g, s0, s1, engine_copy):
-            o = sh_grp[g][:, s0:s1, :].rearrange("p (c i) t -> p c t i", i=4)
-            i = sh_raw[g][:, :, s0:s1].rearrange("p t (c i) -> p c t i", i=4)
-            engine_copy(out=o, in_=i)
-
-        def interleave_on_gpsimd(g):
-            nc.gpsimd.tensor_scalar(out=sh_grp[g][:, 0:GS, :], in0=sh_raw[g][:, :, 0:GS].rearrange("p t s -> p s t"), scalar1=1.0, scalar2=0.0, op0=MULT, op1=ADD)
+        def interleave_shares(g):
+            sh_grp[g] = work.tile([P, S, 4], BF16, name="shg", align_bytes=64, bufs=1)
+            nc.gpsimd.tensor_scalar(out=sh_grp[g][:], in0=sh_raw[g][:].rearrange("p t s -> p s t"), scalar1=1.0, scalar2=0.0, op0=MULT, op1=ADD)
 
         def quantize_shares(g):
             nc.vector.quantize_mx(out=sh_codes[g][:].bitcast(E4M3X4), scales=sh_scales[g][:], in_=sh_grp[g][:].rearrange("p s t -> p (s t)"))
 
-        def second_product(i, s0=0, s1=S, acc=None, groups=range(G2)):
-            acc = acc or bank()
-            for g in groups:
+        def second_product(i, s0=0, s1=S):
+            release()
+            acc = bank()
+            for g in range(G2):
                 nc.tensor.matmul_mx(
                     out=acc[:, 0 : s1 - s0],
                     lhsT=net_codes[i][:, g * P : (g + 1) * P].bitcast(E5M2X4),
@@ -262,117 +251,109 @@ def tile_material_requirements_planning_s9_kernel(tc, orders, inv_words, inv_sca
             return acc
 
         def add_and_store(i, acc, s0=0, s1=S, queue=None):
-            res = work.tile([P, s1 - s0], F32, name="res", bufs=MT + 3)
+            res = work.tile([P, s1 - s0], F32, name="res", bufs=RESB)
             nc.vector.tensor_tensor(out=res[:], in0=acc[:, 0 : s1 - s0], in1=con_sb[:, s0:s1], op=ADD)
             (queue or nc.sync).dma_start(out=out[i * P : (i + 1) * P, s0:s1], in_=res[:])
 
+        def clear_plane(h, engine):
+            engine.memset(planes[h][:].rearrange("p g n -> p (g n)").bitcast(I32), 0)
 
-        nc.vector.memset(planes[0][:].rearrange("p g n -> p (g n)").bitcast(I32), 0)
+        def warm_operands():
+            nc.gpsimd.memset(sh_codes[G2 - 1][:, 0:WN], 0)
+            nc.gpsimd.memset(sh_scales[G2 - 1][:, 0:WN].bitcast(I32), 0)
+            nc.gpsimd.memset(net_codes[MT - 1][:, 0:P], 0)
+            nc.gpsimd.memset(net_scales[MT - 1][:, 0:P].bitcast(I32), 0)
 
-        for plane in planes[1:]:
-            nc.vector.memset(plane[:].rearrange("p g n -> p (g n)").bitcast(I32), 0)
+        def warm_passes(n):
+            acc = bank()
+            for j in range(n):
+                nc.tensor.matmul_mx(
+                    out=acc[:, 0:WN],
+                    lhsT=net_codes[MT - 1][:, 0:P].bitcast(E5M2X4),
+                    lhsT_scale=net_scales[MT - 1][:, 0:P],
+                    rhs=sh_codes[G2 - 1][:, 0:WN].bitcast(E4M3X4),
+                    rhs_scale=sh_scales[G2 - 1][:, 0:WN],
+                    start=True,
+                    stop=True,
+                )
+
+        if WARM1:
+            warm_operands()
         make_identity(nc, ident[:])
-        load_orders(0, 0, KP)
-        load_orders(0, KP, K1)
-        load_orders(1)
-        load_inv(0)
-        load_scales(0)
-        load_inv(1)
-        load_orders(2)
-        load_orders(3)
-        load_scales(1)
-        load_inv(2)
-        load_stock(0, 0, HALF)
-        load_inv(3)
-        load_stock(1, 0, HALF)
-        load_stock(0, HALF, C)
-        load_stock(1, HALF, C)
-        load_orders(4)
-        load_orders(5)
-        load_shares(0)
-        load_stock(2)
-        load_orders(6)
-        load_orders(7)
-        load_stock(3)
-        load_shares(1)
-        load_stock(4)
-        load_shares(2)
-        load_stock(5)
-        load_shares(3)
-        load_stock(6)
-        load_stock(7)
+        for h in range(len(PIECES)):
+            clear_plane(h, nc.gpsimd if h < 2 else nc.vector)
+        loads = {
+            "o": load_orders, "i": load_inv, "c": load_scales, "s": load_shares, "k": load_stock,
+            "a": lambda i: load_stock(i, 0, HALF), "b": lambda i: load_stock(i, HALF, C),
+        }
+        for x in LOADS.split():
+            loads[x[0]](int(x[1]))
         nc.sync.dma_start(out=con_sb[:], in_=contract.partition_broadcast(P))
 
-        first = [bank() for j in range(4)]
-        wb = first[3]
+        if WARM1:
+            warm_passes(WARM1)
+        for x in range(HEAD):
+            sort_orders(x, nc.vector.tensor_copy)
+            if x == 2 and WARM2:
+                warm_passes(WARM2)
+            if x < BYPASS:
+                turn_sorted_by_pass(x)
+            else:
+                turn_sorted(x)
+        for x in range(HEAD):
+            if x < BYPASS:
+                quantize_orders(x, 0, 1)
+                quantize_orders(x, 1, 2)
+            else:
+                quantize_orders(x)
+        groups = [(i, c) for c in range(2) for i in range(HEAD)] + [(i, c) for i in range(HEAD, MT) for c in range(2)] + [(i, c) for i in range(MT) for c in range(2, 4)]
+        halves = [(int(x[1]), "ab".index(x[0])) for x in HALVES.split()]
+        done = []
 
-        new_og(0)
-        orders_half(0, 0, nc.scalar.copy, first[0])
-        orders_half(0, 1, nc.vector.tensor_copy, first[1])
-        orders_tile(1, None, first[2])
+        def subtract_up_to(j):
+            while len(done) < j:
+                subtract_stock(*groups[len(done)])
+                done.append(1)
+                for x in AFTER_SUB.get(len(done), "").split():
+                    calls[x[0]](int(x[1]))
 
-        quantize_orders(0, 0, 1)
-        quantize_orders(0, 1, 2)
-        quantize_orders(1)
-        new_net(0)
-        new_net(1)
-        a = {(x, c): first_product(x, c, wb if x + c == 0 else None) for x in range(2) for c in range(2)}
-        for i in (2, 3):
-            sort_orders(i, nc.scalar.copy)
-        for i in (2, 3):
-            sorted_tile(i)
-        for c in range(2):
-            subtract_stock(0, c, a[0, c])
-        quantize_orders(2)
-        b = {(x, c): first_product(x, c) for c in range(2, 4) for x in range(2)}
-        for c in range(2):
-            subtract_stock(1, c, a[1, c])
-        quantize_orders(3)
-        for i in (4, 5):
-            sort_orders(i, nc.scalar.copy)
-        for c in range(2, 4):
-            for x in range(2):
-                subtract_stock(x, c, b[x, c])
-
-        def group(g):
-            for i in (2 * g + 4, 2 * g + 5):
-                if i < MT:
-                    quantize_orders(i)
-            for k in QNG.get(g, ()):
-                quantize_net(k)
+        def window(g):
             quantize_shares(g)
-            if g < G2 - 1:
-                new_grp(g + 1)
-                interleave_on_gpsimd(g + 1)
+            if g + 1 < G2:
+                interleave_shares(g + 1)
 
-        halves = [(n, h) for n in range(MT) for h in range(2)]
-        new_grp(0)
-        interleave_on_gpsimd(0)
-        for i in range(2, MT):
-            new_net(i)
-            for c in range(G2):
-                gross(i, c)
-                if (i, c) in QG:
-                    group(QG[i, c])
-                for k in QN.get((i, c), ()):
-                    quantize_net(k)
-            if i < 4:
-                for j in (2 * i, 2 * i + 1):
-                    sorted_tile(j)
-            if (i, 4) in QG:
-                group(QG[i, 4])
-            if i == 2:
-                for j in (6, 7):
-                    sort_orders(j, nc.scalar.copy)
-            for n, h in halves[HV[i - 2] : HV[i - 1]]:
-                relu_net(n, h, turn_net(n, h))
-
+        calls = {"o": quantize_orders, "a": lambda i: quantize_net(i, 0), "b": lambda i: quantize_net(i, 1), "w": quantize_shares, "x": interleave_on_scalar, "s": lambda i: sort_orders(i, nc.vector.tensor_copy), "g": interleave_shares}
+        for x in SORT_AFTER.get(0, ()):
+            sort_orders(x, nc.scalar.copy)
+        taken = 0
+        for j, (i, c) in enumerate(groups):
+            subtract_up_to(j - LAG)
+            first_product(i, c)
+            if j + 1 in RUNS:
+                tiles, nh = RUNS[j + 1]
+                for x in tiles:
+                    turn_sorted(x)
+                for n, h in halves[taken : taken + nh]:
+                    turn_net(n, h)
+                taken = taken + nh
+                for x in SORT_AFTER.get(j + 1, ()):
+                    sort_orders(x, nc.scalar.copy)
+                for x in AFTER_RUN.get(j + 1, "").split():
+                    calls[x[0]](int(x[1]))
+        subtract_up_to(len(groups))
         for n in range(0, MT - 2):
             acc = second_product(n)
-            for k in QT.get(n, ()):
-                quantize_net(k)
+            for x in QT.get(n, "").split():
+                calls[x[0]](int(x[1]))
             add_and_store(n, acc)
-            for k in TT.get(n, ()):
-                net_tile(k)
+            if n == LAST_RUN:
+                for x, h in halves[taken:]:
+                    turn_net(x, h)
+                for x in AFTER_LAST.split():
+                    calls[x[0]](int(x[1]))
         for n, s0, s1, q in ((6, 0, 256, nc.sync), (6, 256, 512, nc.sync), (7, 0, 256, nc.sync), (7, 256, 384, nc.scalar), (7, 384, 512, nc.sync)):
-            add_and_store(n, second_product(n, s0, s1), s0, s1, q)
+            acc = second_product(n, s0, s1)
+            if (n, s0) == (6, 0):
+                for x in QT.get(6, "").split():
+                    calls[x[0]](int(x[1]))
+            add_and_store(n, acc, s0, s1, q)

@@ -34,19 +34,21 @@ WN = 512
 WARM1 = 0
 WARM2 = 0
 HEAD = 4
-BYPASS = 1
+BYPASS = 4
 GATE_TILE = 7
-LOADS = 'o0 o1 o2 o3 i0 c0 o4 o5 i1 c1 a0 a1 a2 a3 o6 o7 a4 a5 s0 i2 c2 a6 i3 a7 s1 b0 s2 b1 b2 b3 s3 b4 b5 b6 b7'
-HALVES = "a0 a1 a2 a3 b0 a4 a5 a6 a7 b1 b2 b3 b4 b5 b6 b7"
+LOADS = 'o0 o1 o2 o3 i0 c0 o4 o5 i1 c1 a0 a1 a2 a3 o6 o7 a4 a5 s0 i2 c2 a6 s1 i3 a7 b0 s2 b1 b2 b3 s3 b4 b5 b6 b7'
+HALVES = "a0 a1 a2 a3 a4 a5 a6 a7 b0 b1 b2 b3 b4 b5 b6 b7"
 LAG = 1
-RUNS = {4: ((4, 5), 0), 10: ((6, 7), 4), 22: ((), 5)}
+RUNS = {4: ((4, 5), 0), 10: ((6, 7), 2), 16: ((), 4), 22: ((), 4), 28: ((), 3)}
 SORT_AFTER = {0: (4, 5), 4: (6, 7)}
 AFTER_RUN = {10: 'x1'}
-AFTER_SUB = {3: 'o4', 4: 'o5', 10: 'o6 o7 g0', 16: 'a0 w0 g2', 22: 'a1 w1 w2 g3', 28: 'b0 w3'}
-QT = {1: 'b2 a4', 2: 'b3 a5', 3: 'b4 a6', 4: 'b5 a7', 5: 'b6', 6: 'b7'}
-AFTER_LAST = 'a2 b1 a3'
-LAST_RUN = 0
+AFTER_SUB = {4: 'o4 o5', 10: 'o6 o7 g0', 16: 'a0 w0 g2', 22: 'a1 w1 w2 g3', 28: 'b0 w3', 30: 'b1', 32: 'a2'}
+QT = {0: 'b2 a3', 1: 'b3 a4', 2: 'b4 a6', 3: 'b5 a7', 4: 'b6', 5: 'b7'}
+AFTER_LAST = 'a5'
+LAST_RUN = 1
 HOLD = 2
+EARLY = 8
+W2AT = 1
 
 
 def tile_material_requirements_planning_s9_kernel(tc, orders, inv_words, inv_scales, stock, shares, contract, out):
@@ -259,42 +261,41 @@ def tile_material_requirements_planning_s9_kernel(tc, orders, inv_words, inv_sca
             engine.memset(planes[h][:].rearrange("p g n -> p (g n)").bitcast(I32), 0)
 
         def warm_operands():
-            nc.gpsimd.memset(sh_codes[G2 - 1][:, 0:WN], 0)
-            nc.gpsimd.memset(sh_scales[G2 - 1][:, 0:WN].bitcast(I32), 0)
-            nc.gpsimd.memset(net_codes[MT - 1][:, 0:P], 0)
-            nc.gpsimd.memset(net_scales[MT - 1][:, 0:P].bitcast(I32), 0)
+            nc.vector.memset(inv_sb[G2 - 1][:, 0, :].bitcast(I32), 0)
+            nc.vector.memset(ord_codes[MT - 1][:, 0:P], 0)
 
         def warm_passes(n):
+            release()
             acc = bank()
             for j in range(n):
                 nc.tensor.matmul_mx(
-                    out=acc[:, 0:WN],
-                    lhsT=net_codes[MT - 1][:, 0:P].bitcast(E5M2X4),
-                    lhsT_scale=net_scales[MT - 1][:, 0:P],
-                    rhs=sh_codes[G2 - 1][:, 0:WN].bitcast(E4M3X4),
-                    rhs_scale=sh_scales[G2 - 1][:, 0:WN],
+                    out=acc[:],
+                    lhsT=ord_codes[MT - 1][:, 0:P].bitcast(E4M3X4),
+                    lhsT_scale=planes[-1][:, 1, 0:P],
+                    rhs=inv_sb[G2 - 1][:, 0, :].bitcast(E2M1X4),
+                    rhs_scale=planes[-1][:, 0, 0:N],
                     start=True,
                     stop=True,
                 )
 
+        make_identity(nc, ident[:])
+        clear_plane(len(PIECES) - 1, nc.vector)
         if WARM1:
             warm_operands()
-        make_identity(nc, ident[:])
-        for h in range(len(PIECES)):
-            clear_plane(h, nc.gpsimd if h < 2 else nc.vector)
+        for h in range(len(PIECES) - 1):
+            clear_plane(h, nc.vector)
         loads = {
             "o": load_orders, "i": load_inv, "c": load_scales, "s": load_shares, "k": load_stock,
             "a": lambda i: load_stock(i, 0, HALF), "b": lambda i: load_stock(i, HALF, C),
         }
-        for x in LOADS.split():
+        for x in LOADS.split()[:EARLY]:
             loads[x[0]](int(x[1]))
-        nc.sync.dma_start(out=con_sb[:], in_=contract.partition_broadcast(P))
 
         if WARM1:
             warm_passes(WARM1)
         for x in range(HEAD):
             sort_orders(x, nc.vector.tensor_copy)
-            if x == 2 and WARM2:
+            if x == W2AT and WARM2:
                 warm_passes(WARM2)
             if x < BYPASS:
                 turn_sorted_by_pass(x)
@@ -306,6 +307,9 @@ def tile_material_requirements_planning_s9_kernel(tc, orders, inv_words, inv_sca
                 quantize_orders(x, 1, 2)
             else:
                 quantize_orders(x)
+        for x in LOADS.split()[EARLY:]:
+            loads[x[0]](int(x[1]))
+        nc.sync.dma_start(out=con_sb[:], in_=contract.partition_broadcast(P))
         groups = [(i, c) for c in range(2) for i in range(HEAD)] + [(i, c) for i in range(HEAD, MT) for c in range(2)] + [(i, c) for i in range(MT) for c in range(2, 4)]
         halves = [(int(x[1]), "ab".index(x[0])) for x in HALVES.split()]
         done = []

@@ -225,10 +225,7 @@ def tile_material_requirements_planning_s9_kernel(tc, orders, inv_words, inv_sca
 
         def interleave_on_scalar(g):
             sh_grp[g] = work.tile([P, S, 4], BF16, name="shx", align_bytes=64, bufs=1)
-            nc.scalar.copy(
-                out=sh_grp[g][:].rearrange("p (c i) t -> p c t i", i=4),
-                in_=sh_raw[g][:].rearrange("p t (c i) -> p c t i", i=4),
-            )
+            nc.scalar.copy(out=sh_grp[g][:], in_=sh_raw[g][:].rearrange("p t s -> p s t"))
 
         def interleave_shares(g):
             sh_grp[g] = work.tile([P, S, 4], BF16, name="shg", align_bytes=64, bufs=1)

@@ -35,14 +35,14 @@ WARM1 = 0
 WARM2 = 0
 HEAD = 4
 BYPASS = 4
-GATE_TILE = 7
-LOADS = 'o0 o1 o2 o3 i0 c0 o4 o5 i1 c1 a0 a1 a2 a3 o6 o7 a4 a5 s0 i2 c2 a6 s1 i3 a7 b0 s2 b1 b2 b3 s3 b4 b5 b6 b7'
+GATE_TILE = 5
+LOADS = 'o0 o1 o2 o3 i0 c0 o4 o5 i1 c1 a0 a1 a2 a3 o6 s0 o7 a4 a5 a6 s1 i2 c2 a7 i3 b0 b1 s2 b2 b3 b4 s3 b5 b6 b7'
 HALVES = "a0 a1 a2 a3 a4 a5 a6 a7 b0 b1 b2 b3 b4 b5 b6 b7"
 LAG = 1
 RUNS = {4: ((4, 5), 0), 10: ((6, 7), 2), 16: ((), 4), 22: ((), 4), 28: ((), 3)}
 SORT_AFTER = {0: (4, 5), 4: (6, 7)}
-AFTER_RUN = {10: 'x1'}
-AFTER_SUB = {4: 'o4 o5', 10: 'o6 o7 g0', 16: 'a0 w0 g2', 22: 'a1 w1 w2 g3', 28: 'b0 w3', 30: 'b1', 32: 'a2'}
+AFTER_RUN = {}
+AFTER_SUB = {4: 'o4 o5 g0', 10: 'o6 o7 w0 g1', 16: 'a0 w1 g2', 22: 'a1 w2 g3', 28: 'b0 w3', 30: 'b1', 32: 'a2'}
 QT = {0: 'b2 a3', 1: 'b3 a4', 2: 'b4 a6', 3: 'b5 a7', 4: 'b6', 5: 'b7'}
 AFTER_LAST = 'a5'
 LAST_RUN = 1

@@ -39,14 +39,14 @@ GATE_TILE = 5
 LOADS = 'o0 o1 o2 o3 i0 c0 o4 o5 i1 c1 a0 a1 a2 a3 o6 s0 o7 a4 a5 a6 s1 i2 c2 a7 i3 b0 b1 s2 b2 b3 b4 s3 b5 b6 b7'
 HALVES = "a0 a1 a2 a3 a4 a5 a6 a7 b0 b1 b2 b3 b4 b5 b6 b7"
 LAG = 1
-RUNS = {4: ((4, 5), 0), 10: ((6, 7), 2), 16: ((), 4), 22: ((), 4), 28: ((), 3)}
+RUNS = {4: ((4, 5), 0), 9: ((6, 7), 1), 14: ((), 3), 19: ((), 3), 24: ((), 3), 29: ((), 3)}
 SORT_AFTER = {0: (4, 5), 4: (6, 7)}
 AFTER_RUN = {}
-AFTER_SUB = {4: 'o4 o5 g0', 10: 'o6 o7 w0 g1', 16: 'a0 w1 g2', 22: 'a1 w2 g3', 28: 'b0 w3', 30: 'b1', 32: 'a2'}
+AFTER_SUB = {3: 'o4 o5 g0', 9: 'o6 o7 w0 g1', 15: 'a0 w1 g2', 21: 'a1 w2 g3', 27: 'b0 w3', 30: 'b1', 32: 'a2'}
 QT = {0: 'b2 a3', 1: 'b3 a4', 2: 'b4 a6', 3: 'b5 a7', 4: 'b6', 5: 'b7'}
 AFTER_LAST = 'a5'
 LAST_RUN = 1
-HOLD = 2
+HOLD = 0
 EARLY = 8
 W2AT = 1
 
@@ -152,6 +152,24 @@ def tile_material_requirements_planning_s9_kernel(tc, orders, inv_words, inv_sca
                 in_=ord_sb[i][:].bitcast(F32).rearrange("m (x u) -> m u x", u=2),
             )
 
+        def sort_pass(i, g, engine_copy):
+            if g == 0:
+                srt[i] = work.tile([P, K1 // 2], F32, name="srt", align_bytes=64, bufs=4)
+            engine_copy(
+                out=srt[i][:, g * 256 : (g + 1) * 256].rearrange("m (u x) -> m u x", u=2),
+                in_=ord_sb[i][:, g * KP : (g + 1) * KP].bitcast(F32).rearrange("m (x u) -> m u x", u=2),
+            )
+
+        def turn_pass_sorted(i):
+            new_og(i)
+            t = bank()
+            for j in range(4):
+                nc.tensor.transpose(t[:, j * P : (j + 1) * P], srt[i][:, j * P : (j + 1) * P], ident[:])
+            nc.scalar.copy(
+                out=og[i][:].bitcast(F32).rearrange("p (g m u) -> p g m u", g=G1, u=2),
+                in_=t[:].rearrange("p (g u m) -> p g m u", g=G1, u=2),
+            )
+
         def turn_sorted(i, engine_copy=nc.scalar.copy):
             new_og(i)
             t = bank()
@@ -223,6 +241,10 @@ def tile_material_requirements_planning_s9_kernel(tc, orders, inv_words, inv_sca
                 in_=ng[i, h][:],
             )
 
+        def quantize_whole(i):
+            quantize_net(i, 0)
+            quantize_net(i, 1)
+
         def interleave_on_scalar(g):
             sh_grp[g] = work.tile([P, S, 4], BF16, name="shx", align_bytes=64, bufs=1)
             nc.scalar.copy(out=sh_grp[g][:], in_=sh_raw[g][:].rearrange("p t s -> p s t"))
@@ -234,10 +256,11 @@ def tile_material_requirements_planning_s9_kernel(tc, orders, inv_words, inv_sca
         def quantize_shares(g):
             nc.vector.quantize_mx(out=sh_codes[g][:].bitcast(E4M3X4), scales=sh_scales[g][:], in_=sh_grp[g][:].rearrange("p s t -> p (s t)"))
 
-        def second_product(i, s0=0, s1=S):
-            release()
-            acc = bank()
-            for g in range(G2):
+        def second_product(i, s0=0, s1=S, acc=None, passes=range(G2)):
+            if acc is None:
+                release()
+                acc = bank()
+            for g in passes:
                 nc.tensor.matmul_mx(
                     out=acc[:, 0 : s1 - s0],
                     lhsT=net_codes[i][:, g * P : (g + 1) * P].bitcast(E5M2X4),
@@ -258,6 +281,7 @@ def tile_material_requirements_planning_s9_kernel(tc, orders, inv_words, inv_sca
             engine.memset(planes[h][:].rearrange("p g n -> p (g n)").bitcast(I32), 0)
 
         def warm_operands():
+            nc.vector.memset(planes[-1][:, 0, 0:N].bitcast(I32), 0)
             nc.vector.memset(inv_sb[G2 - 1][:, 0, :].bitcast(I32), 0)
             nc.vector.memset(ord_codes[MT - 1][:, 0:P], 0)
 
@@ -268,7 +292,7 @@ def tile_material_requirements_planning_s9_kernel(tc, orders, inv_words, inv_sca
                 nc.tensor.matmul_mx(
                     out=acc[:],
                     lhsT=ord_codes[MT - 1][:, 0:P].bitcast(E4M3X4),
-                    lhsT_scale=planes[-1][:, 1, 0:P],
+                    lhsT_scale=planes[-1][:, 0, 0:P],
                     rhs=inv_sb[G2 - 1][:, 0, :].bitcast(E2M1X4),
                     rhs_scale=planes[-1][:, 0, 0:N],
                     start=True,

@@ -33,22 +33,23 @@ RESB = 9
 WN = 512
 WARM1 = 0
 WARM2 = 0
-HEAD = 4
+HEAD = 3
 BYPASS = 4
 GATE_TILE = 5
-LOADS = 'o0 o1 o2 o3 i0 c0 o4 o5 i1 c1 a0 a1 a2 a3 o6 s0 o7 a4 a5 a6 s1 i2 c2 a7 i3 b0 b1 s2 b2 b3 b4 s3 b5 b6 b7'
+LOADS = 'o1 o2 i0 c0 o3 o4 o5 i1 c1 a0 a1 a2 s0 o6 o7 a3 a4 a5 s1 a6 i2 c2 a7 i3 b0 b1 s2 b2 b3 b4 s3 b5 b6 b7'
 HALVES = "a0 a1 a2 a3 a4 a5 a6 a7 b0 b1 b2 b3 b4 b5 b6 b7"
 LAG = 1
-RUNS = {4: ((4, 5), 0), 9: ((6, 7), 1), 14: ((), 3), 19: ((), 3), 24: ((), 3), 29: ((), 3)}
-SORT_AFTER = {0: (4, 5), 4: (6, 7)}
+RUNS = {3: ((3, 4, 5), 0), 9: ((6, 7), 1), 14: ((), 3), 19: ((), 3), 24: ((), 3), 29: ((), 3)}
+SORT_AFTER = {0: (3, 4, 5), 3: (6, 7)}
 AFTER_RUN = {}
-AFTER_SUB = {3: 'o4 o5 g0', 9: 'o6 o7 w0 g1', 15: 'a0 w1 g2', 21: 'a1 w2 g3', 27: 'b0 w3', 30: 'b1', 32: 'a2'}
+AFTER_SUB = {2: 'o3', 3: 'o4 o5 g0', 9: 'o6 o7 w0 g1', 15: 'a0 w1 g2', 21: 'a1 w2 g3', 27: 'b0 w3', 30: 'b1', 32: 'a2'}
 QT = {0: 'b2 a3', 1: 'b3 a4', 2: 'b4 a6', 3: 'b5 a7', 4: 'b6', 5: 'b7'}
 AFTER_LAST = 'a5'
 LAST_RUN = 1
 HOLD = 0
-EARLY = 8
+EARLY = 4
 W2AT = 1
+BLOCKS = ((0, 1, 2), (3,), (4,), (5,), (6,), (7,))
 
 
 def tile_material_requirements_planning_s9_kernel(tc, orders, inv_words, inv_scales, stock, shares, contract, out):
@@ -300,7 +301,6 @@ def tile_material_requirements_planning_s9_kernel(tc, orders, inv_words, inv_sca
                 )
 
         make_identity(nc, ident[:])
-        clear_plane(len(PIECES) - 1, nc.vector)
         if WARM1:
             warm_operands()
         for h in range(len(PIECES) - 1):
@@ -309,29 +309,27 @@ def tile_material_requirements_planning_s9_kernel(tc, orders, inv_words, inv_sca
             "o": load_orders, "i": load_inv, "c": load_scales, "s": load_shares, "k": load_stock,
             "a": lambda i: load_stock(i, 0, HALF), "b": lambda i: load_stock(i, HALF, C),
         }
+        load_orders(0, 0, KP)
+        load_orders(0, KP, K1)
         for x in LOADS.split()[:EARLY]:
             loads[x[0]](int(x[1]))
 
         if WARM1:
             warm_passes(WARM1)
-        for x in range(HEAD):
+        new_og(0)
+        for g in range(G1):
+            orders_half(0, g, nc.scalar.copy)
+        for x in range(1, HEAD):
             sort_orders(x, nc.vector.tensor_copy)
-            if x == W2AT and WARM2:
-                warm_passes(WARM2)
-            if x < BYPASS:
-                turn_sorted_by_pass(x)
-            else:
-                turn_sorted(x)
+            turn_sorted_by_pass(x)
         for x in range(HEAD):
-            if x < BYPASS:
-                quantize_orders(x, 0, 1)
-                quantize_orders(x, 1, 2)
-            else:
-                quantize_orders(x)
+            for g in range(G1):
+                quantize_orders(x, g, g + 1)
+        clear_plane(len(PIECES) - 1, nc.vector)
         for x in LOADS.split()[EARLY:]:
             loads[x[0]](int(x[1]))
         nc.sync.dma_start(out=con_sb[:], in_=contract.partition_broadcast(P))
-        groups = [(i, c) for c in range(2) for i in range(HEAD)] + [(i, c) for i in range(HEAD, MT) for c in range(2)] + [(i, c) for i in range(MT) for c in range(2, 4)]
+        groups = [(i, c) for b in BLOCKS for c in range(2) for i in b] + [(i, c) for i in range(MT) for c in range(2, 4)]
         halves = [(int(x[1]), "ab".index(x[0])) for x in HALVES.split()]
         done = []
 
@@ -347,7 +345,7 @@ def tile_material_requirements_planning_s9_kernel(tc, orders, inv_words, inv_sca
             if g + 1 < G2:
                 interleave_shares(g + 1)
 
-        calls = {"o": quantize_orders, "a": lambda i: quantize_net(i, 0), "b": lambda i: quantize_net(i, 1), "w": quantize_shares, "x": interleave_on_scalar, "s": lambda i: sort_orders(i, nc.vector.tensor_copy), "g": interleave_shares}
+        calls = {"o": quantize_orders, "a": lambda i: quantize_net(i, 0), "b": lambda i: quantize_net(i, 1), "w": quantize_shares, "x": interleave_on_scalar, "s": lambda i: sort_orders(i, nc.vector.tensor_copy), "g": interleave_shares, "p": lambda i: quantize_orders(i, 0, 1), "q": lambda i: quantize_orders(i, 1, 2)}
         for x in SORT_AFTER.get(0, ()):
             sort_orders(x, nc.scalar.copy)
         taken = 0

@@ -93,6 +93,9 @@ def tile_material_requirements_planning_s9_kernel(tc, orders, inv_words, inv_sca
                 in_=inv_words.rearrange("g p b -> p g b")[:, :, 2 * N * c : 2 * N * (c + 1)].bitcast(I32),
             )
 
+        def load_inv_pass(g):
+            nc.sync.dma_start(out=inv_sb[0][:, g, :].bitcast(I32), in_=inv_words[g][:, 0 : 2 * N].bitcast(I32))
+
         def load_scales(h):
             rows = inv_scales.rearrange("g (q r) n -> r q g n", r=4)
             for r in range(4):
@@ -309,8 +312,7 @@ def tile_material_requirements_planning_s9_kernel(tc, orders, inv_words, inv_sca
             "o": load_orders, "i": load_inv, "c": load_scales, "s": load_shares, "k": load_stock,
             "a": lambda i: load_stock(i, 0, HALF), "b": lambda i: load_stock(i, HALF, C),
         }
-        load_orders(0, 0, KP)
-        load_orders(0, KP, K1)
+        load_orders(0)
         for x in LOADS.split()[:EARLY]:
             loads[x[0]](int(x[1]))
 

@@ -21,35 +21,33 @@ RELU = mybir.ActivationFunctionType.Relu
 
 P = 128
 KP = 512
+N = 512
 MT = M // P
 G1 = K1 // KP
 G2 = C // KP
-N = 512
 HALF = C // 2
+BANKS = 8
 PIECES = ((0, 1), (1, 2), (2, 4))
-NETB = 8
-NGB = 16
-RESB = 9
-WN = 512
-WARM1 = 0
-WARM2 = 0
+AT_MOVING_CODES, AT_STILL_CODES, AT_MOVING_SCALES, AT_STILL_SCALES = 0, 128, 128, 128
 HEAD = 3
-BYPASS = 4
 GATE_TILE = 5
-LOADS = 'o1 o2 i0 c0 o3 o4 o5 i1 c1 a0 a1 a2 s0 o6 o7 a3 a4 a5 s1 a6 i2 c2 a7 i3 b0 b1 s2 b2 b3 b4 s3 b5 b6 b7'
-HALVES = "a0 a1 a2 a3 a4 a5 a6 a7 b0 b1 b2 b3 b4 b5 b6 b7"
 LAG = 1
-RUNS = {3: ((3, 4, 5), 0), 9: ((6, 7), 1), 14: ((), 3), 19: ((), 3), 24: ((), 3), 29: ((), 3)}
-SORT_AFTER = {0: (3, 4, 5), 3: (6, 7)}
-AFTER_RUN = {}
-AFTER_SUB = {2: 'o3', 3: 'o4 o5 g0', 9: 'o6 o7 w0 g1', 15: 'a0 w1 g2', 21: 'a1 w2 g3', 27: 'b0 w3', 30: 'b1', 32: 'a2'}
-QT = {0: 'b2 a3', 1: 'b3 a4', 2: 'b4 a6', 3: 'b5 a7', 4: 'b6', 5: 'b7'}
-AFTER_LAST = 'a5'
+CLEAR_FIRST = "Z0 Z1"
+CLEAR_LATER = "Z2"
+FIRST_LOADS = "o0 o1 o2 i0 c0"
+LOADS = "o3 o4 o5 i1 c1 a0 a1 a2 s0 o6 o7 a3 a4 a5 s1 a6 i2 c2 a7 i3 b0 b1 s2 b2 b3 b4 s3 b5 b6 b7"
+FIRST_GROUPS = [(0, 0), (1, 0), (2, 0), (0, 1), (1, 1), (2, 1)]
+FIRST_SUBS = []
+RUNS = (3, 9, 14, 19, 24, 29)
+SORTS = {0: "S3 S4 S5", 3: "S6 S7"}
+AFTER_SUB = {2: "O3", 3: "O4 O5 G0", 9: "O6 O7 W0 G1", 15: "A0 W1 G2", 21: "A1 W2 G3", 27: "B0 W3", 30: "B1", 32: "A2"}
+QT = {0: "B2 A3", 1: "B3 A4", 2: "B4 A6", 3: "B5 A7", 4: "B6", 5: "B7"}
+AFTER_LAST = "A5"
 LAST_RUN = 1
-HOLD = 0
-EARLY = 4
-W2AT = 1
-BLOCKS = ((0, 1, 2), (3,), (4,), (5,), (6,), (7,))
+HELD = 0
+LATE_RELU = ()
+TURNS = "o3 o4 o5 o6 o7 a0 a1 a2 a3 a4 a5 a6 a7 b0 b1 b2 b3 b4 b5 b6 b7"
+FIRST_SUB_AT = 3
 
 
 def tile_material_requirements_planning_s9_kernel(tc, orders, inv_words, inv_scales, stock, shares, contract, out):
@@ -67,34 +65,48 @@ def tile_material_requirements_planning_s9_kernel(tc, orders, inv_words, inv_sca
             return flat.rearrange("p (g n) -> p g n", g=shape[1]) if len(shape) == 3 else flat
 
         ident = keep.tile([P, P], F32, name="ident")
-        planes = [placed([P, G1, (b - a) * N], U8, 1, "planes%d" % a, 128) for a, b in PIECES]
-        inv_sb = [placed([P, G1, 2 * N], U8, 1, "inv%d" % c, 0) for c in range(G2)]
+        planes = [placed([P, G1, (b - a) * N], U8, 1, "planes%d" % a, AT_MOVING_SCALES) for a, b in PIECES]
+        inv_sb = [placed([P, G1, 2 * N], U8, 1, "inv%d" % c, AT_MOVING_CODES) for c in range(G2)]
         ord_sb = [keep.tile([P, K1], BF16, name="ord%d" % i, align_bytes=64) for i in range(MT)]
-        stk_sb = [keep.tile([P, C], BF16, name="stk%d" % i, align_bytes=64) for i in range(MT)]
+        stk_first = [keep.tile([P, HALF], BF16, name="stka%d" % i, align_bytes=64) for i in range(MT)]
+        stk_pair = [keep.tile([P, 2 * HALF], BF16, name="stkb%d" % j, align_bytes=64) for j in range(MT // 2)]
+        stk = {}
+        for i in range(MT):
+            stk[i, 0] = stk_first[i][:]
+            stk[i, 1] = stk_pair[i // 2][:, i % 2 * HALF : (i % 2 + 1) * HALF]
         sh_raw = [keep.tile([P, 4, S], BF16, name="shr%d" % g, align_bytes=64) for g in range(G2)]
-        sh_codes = [placed([P, S], U32, 4, "shc%d" % g, 0) for g in range(G2)]
-        sh_scales = [placed([P, S], U8, 1, "shs%d" % g, 128) for g in range(G2)]
-        ord_codes = [placed([P, G1 * P], U32, 4, "oc%d" % i, 64) for i in range(MT)]
-        ord_scales = [placed([P, G1 * P], U8, 1, "os%d" % i, 128) for i in range(MT)]
-        net_codes = [placed([P, G2 * P], U32, 4, "nc%d" % i, 64) for i in range(MT)]
-        net_scales = [placed([P, G2 * P], U8, 1, "ns%d" % i, 128) for i in range(MT)]
+        sh_codes = [placed([P, S], U32, 4, "shc%d" % g, AT_MOVING_CODES) for g in range(G2)]
+        sh_scales = [placed([P, S], U8, 1, "shs%d" % g, AT_MOVING_SCALES) for g in range(G2)]
+        ord_codes = [placed([P, G1 * P], U32, 4, "oc%d" % i, AT_STILL_CODES) for i in range(MT)]
+        ord_scales = [placed([P, G1 * P], U8, 1, "os%d" % i, AT_STILL_SCALES) for i in range(MT)]
+        net_codes = [placed([P, G2 * P], U32, 4, "nc%d" % i, AT_STILL_CODES) for i in range(MT)]
+        net_scales = [placed([P, G2 * P], U8, 1, "ns%d" % i, AT_STILL_SCALES) for i in range(MT)]
         con_sb = keep.tile([P, S], BF16, name="con", align_bytes=64)
-        sh_grp, og, nets, ng, srt, acc1 = {}, {}, {}, {}, {}, {}
+        sh_grp, og, nets, ng, srt, acc1, turned = {}, {}, {}, {}, {}, {}, {}
+        ring, held = list(range(BANKS)), []
 
-        def load_orders(i, c0=0, c1=K1):
-            nc.sync.dma_start(out=ord_sb[i][:, c0:c1], in_=orders[i * P : (i + 1) * P, c0:c1])
+        def bank(hold=False):
+            b = ring.pop(0)
+            (held if hold else ring).append(b)
+            return psum.tile([P, N], F32, name="bank%d" % b)
 
-        def load_stock(i, c0=0, c1=C):
-            nc.sync.dma_start(out=stk_sb[i][:, c0:c1], in_=stock[i * P : (i + 1) * P, c0:c1])
+        def load_orders(i):
+            nc.sync.dma_start(out=ord_sb[i][:], in_=orders[i * P : (i + 1) * P, :])
+
+        def load_stock(i, c0, c1):
+            nc.sync.dma_start(out=stk[i, c0 // HALF][:, c0 % HALF : c0 % HALF + c1 - c0], in_=stock[i * P : (i + 1) * P, c0:c1])
+
+        def load_stock_pair(j):
+            nc.sync.dma_start(
+                out=stk_pair[j][:].rearrange("p (t c) -> p t c", t=2),
+                in_=stock[2 * j * P : 2 * (j + 1) * P, HALF:C].rearrange("(t p) c -> p t c", t=2),
+            )
 
         def load_inv(c):
             nc.sync.dma_start(
                 out=inv_sb[c][:].bitcast(I32),
                 in_=inv_words.rearrange("g p b -> p g b")[:, :, 2 * N * c : 2 * N * (c + 1)].bitcast(I32),
             )
-
-        def load_inv_pass(g):
-            nc.sync.dma_start(out=inv_sb[0][:, g, :].bitcast(I32), in_=inv_words[g][:, 0 : 2 * N].bitcast(I32))
 
         def load_scales(h):
             rows = inv_scales.rearrange("g (q r) n -> r q g n", r=4)
@@ -104,21 +116,8 @@ def tile_material_requirements_planning_s9_kernel(tc, orders, inv_words, inv_sca
         def load_shares(g):
             nc.sync.dma_start(out=sh_raw[g][:], in_=shares[g * KP : (g + 1) * KP, :].rearrange("(p j) s -> p j s", j=4))
 
-        ring, held = list(range(8)), []
-
-        def bank(slow=False):
-            b = ring.pop(0)
-            if slow:
-                held.append([b, HOLD * len(held)])
-            else:
-                ring.append(b)
-                for x in held:
-                    x[1] = x[1] - 1
-            return psum.tile([P, N], F32, name="bank%d" % b)
-
-        def release():
-            while held and held[0][1] <= 0:
-                ring.append(held.pop(0)[0])
+        def clear_plane(h):
+            nc.vector.memset(planes[h][:].rearrange("p g n -> p (g n)").bitcast(I32), 0)
 
         def new_og(i):
             if i == GATE_TILE:
@@ -126,28 +125,15 @@ def tile_material_requirements_planning_s9_kernel(tc, orders, inv_words, inv_sca
             else:
                 og[i] = work.tile([P, K1], BF16, name="og", align_bytes=64, bufs=4)
 
-        def copy_words(engine_copy, dst, t, width):
-            engine_copy(
-                out=dst.bitcast(F32).rearrange("p (x u) -> p x u", u=2),
-                in_=t[:, 0 : 2 * width].rearrange("p (u x) -> p x u", u=2),
-            )
-
-        def turn_unsorted(i, g, t, slot, width):
+        def turn_unsorted_pass(i, g):
+            t = bank()
             words = ord_sb[i][:].bitcast(F32)
             for u in range(2):
-                nc.tensor.transpose(t[:, u * width + slot * P : u * width + (slot + 1) * P], words[:, 256 * g + u : 256 * (g + 1) : 2], ident[:])
-
-        def orders_half(i, g, engine_copy):
-            t = bank()
-            turn_unsorted(i, g, t, 0, P)
-            copy_words(engine_copy, og[i][:, g * KP : (g + 1) * KP], t, P)
-
-        def orders_whole(i, engine_copy):
-            new_og(i)
-            t = bank()
-            for g in range(G1):
-                turn_unsorted(i, g, t, g, 2 * P)
-            copy_words(engine_copy, og[i][:], t, 2 * P)
+                nc.tensor.transpose(t[:, u * P : (u + 1) * P], words[:, 256 * g + u : 256 * (g + 1) : 2], ident[:])
+            nc.scalar.copy(
+                out=og[i][:, g * KP : (g + 1) * KP].bitcast(F32).rearrange("p (m u) -> p m u", u=2),
+                in_=t[:, 0 : 2 * P].rearrange("p (u m) -> p m u", u=2),
+            )
 
         def sort_orders(i, engine_copy):
             srt[i] = work.tile([P, K1 // 2], F32, name="srt", align_bytes=64, bufs=4)
@@ -156,40 +142,16 @@ def tile_material_requirements_planning_s9_kernel(tc, orders, inv_words, inv_sca
                 in_=ord_sb[i][:].bitcast(F32).rearrange("m (x u) -> m u x", u=2),
             )
 
-        def sort_pass(i, g, engine_copy):
-            if g == 0:
-                srt[i] = work.tile([P, K1 // 2], F32, name="srt", align_bytes=64, bufs=4)
-            engine_copy(
-                out=srt[i][:, g * 256 : (g + 1) * 256].rearrange("m (u x) -> m u x", u=2),
-                in_=ord_sb[i][:, g * KP : (g + 1) * KP].bitcast(F32).rearrange("m (x u) -> m u x", u=2),
-            )
-
-        def turn_pass_sorted(i):
+        def turn_orders(i, pieces):
             new_og(i)
             t = bank()
             for j in range(4):
                 nc.tensor.transpose(t[:, j * P : (j + 1) * P], srt[i][:, j * P : (j + 1) * P], ident[:])
-            nc.scalar.copy(
-                out=og[i][:].bitcast(F32).rearrange("p (g m u) -> p g m u", g=G1, u=2),
-                in_=t[:].rearrange("p (g u m) -> p g m u", g=G1, u=2),
-            )
-
-        def turn_sorted(i, engine_copy=nc.scalar.copy):
-            new_og(i)
-            t = bank()
-            for j in range(4):
-                nc.tensor.transpose(t[:, j * P : (j + 1) * P], srt[i][:, j * P : (j + 1) * P], ident[:])
-            copy_words(engine_copy, og[i][:], t, 2 * P)
-
-        def turn_sorted_by_pass(i):
-            new_og(i)
-            t = bank()
-            for j in range(4):
-                nc.tensor.transpose(t[:, j * P : (j + 1) * P], srt[i][:, j * P : (j + 1) * P], ident[:])
-            for g in range(G1):
+            w = 2 * P // pieces
+            for j in range(pieces):
                 nc.scalar.copy(
-                    out=og[i][:, g * KP : (g + 1) * KP].bitcast(F32).rearrange("p (m u) -> p m u", u=2),
-                    in_=t[:].rearrange("p (u g m) -> p g m u", u=2, g=G1)[:, g],
+                    out=og[i][:].bitcast(F32).rearrange("p (x u) -> p x u", u=2)[:, j * w : (j + 1) * w, :],
+                    in_=t[:].rearrange("p (u x) -> p x u", u=2)[:, j * w : (j + 1) * w, :],
                 )
 
         def quantize_orders(i, a=0, b=G1):
@@ -199,10 +161,9 @@ def tile_material_requirements_planning_s9_kernel(tc, orders, inv_words, inv_sca
                 in_=og[i][:, a * KP : b * KP],
             )
 
-        def first_product(i, c):
+        def first_product(i, c, hold):
             h = [j for j, (a, b) in enumerate(PIECES) if a <= c < b][0]
-            release()
-            acc1[i, c] = bank()
+            acc1[i, c] = bank(hold)
             for g in range(G1):
                 nc.tensor.matmul_mx(
                     out=acc1[i, c][:],
@@ -216,27 +177,33 @@ def tile_material_requirements_planning_s9_kernel(tc, orders, inv_words, inv_sca
 
         def subtract_stock(i, c):
             if c % 2 == 0:
-                nets[i, c // 2] = work.tile([P, HALF], BF16, name="net", align_bytes=64, bufs=NETB)
+                nets[i, c // 2] = work.tile([P, HALF], BF16, name="net", align_bytes=64, bufs=8)
             nc.vector.tensor_tensor(
                 out=nets[i, c // 2][:, c % 2 * N : (c % 2 + 1) * N].rearrange("m (u p e) -> m u p e", u=2, e=2),
                 in0=acc1[i, c][:].rearrange("m (p u e) -> m u p e", u=2, e=2),
-                in1=stk_sb[i][:, c * N : (c + 1) * N].rearrange("m (p u e) -> m u p e", u=2, e=2),
+                in1=stk[i, c // 2][:, c % 2 * N : (c % 2 + 1) * N].rearrange("m (p u e) -> m u p e", u=2, e=2),
                 op=SUB,
             )
 
-        def turn_net(i, h, on_vector=False):
-            t = bank(True)
+        def turn_net(i, h):
+            t = bank()
             words = nets[i, h][:].bitcast(F32)
             for cl in range(2):
                 for u in range(2):
                     nc.tensor.transpose(t[:, u * 256 + cl * P : u * 256 + (cl + 1) * P], words[:, 256 * cl + P * u : 256 * cl + P * (u + 1)], ident[:])
-            ng[i, h] = work.tile([P, HALF], BF16, name="ng", align_bytes=64, bufs=NGB)
-            o = ng[i, h][:].rearrange("p (x u e) -> p x u e", u=2, e=2)
-            src = t[:].bitcast(BF16).rearrange("p (u x e) -> p x u e", u=2, e=2)
-            if on_vector:
-                nc.vector.tensor_scalar_max(out=o, in0=src, scalar1=0.0)
-            else:
-                nc.scalar.activation(out=o, in_=src, func=RELU)
+            ng[i, h] = work.tile([P, HALF], BF16, name="ng", align_bytes=64, bufs=16)
+            turned[i, h] = t
+            if (i, h) not in LATE_RELU:
+                relu(i, h)
+
+        def relu(i, h):
+            nc.scalar.activation(out=relu_out(i, h), in_=relu_in(i, h), func=RELU)
+
+        def relu_out(i, h):
+            return ng[i, h][:].rearrange("p (x u e) -> p x u e", u=2, e=2)
+
+        def relu_in(i, h):
+            return turned[i, h][:].bitcast(BF16).rearrange("p (u x e) -> p x u e", u=2, e=2)
 
         def quantize_net(i, h):
             nc.vector.quantize_mx(
@@ -245,14 +212,6 @@ def tile_material_requirements_planning_s9_kernel(tc, orders, inv_words, inv_sca
                 in_=ng[i, h][:],
             )
 
-        def quantize_whole(i):
-            quantize_net(i, 0)
-            quantize_net(i, 1)
-
-        def interleave_on_scalar(g):
-            sh_grp[g] = work.tile([P, S, 4], BF16, name="shx", align_bytes=64, bufs=1)
-            nc.scalar.copy(out=sh_grp[g][:], in_=sh_raw[g][:].rearrange("p t s -> p s t"))
-
         def interleave_shares(g):
             sh_grp[g] = work.tile([P, S, 4], BF16, name="shg", align_bytes=64, bufs=1)
             nc.gpsimd.tensor_scalar(out=sh_grp[g][:], in0=sh_raw[g][:].rearrange("p t s -> p s t"), scalar1=1.0, scalar2=0.0, op0=MULT, op1=ADD)
@@ -260,9 +219,8 @@ def tile_material_requirements_planning_s9_kernel(tc, orders, inv_words, inv_sca
         def quantize_shares(g):
             nc.vector.quantize_mx(out=sh_codes[g][:].bitcast(E4M3X4), scales=sh_scales[g][:], in_=sh_grp[g][:].rearrange("p s t -> p (s t)"))
 
-        def second_product(i, s0=0, s1=S, acc=None, passes=range(G2)):
+        def second_product(i, s0=0, s1=S, passes=range(G2), acc=None):
             if acc is None:
-                release()
                 acc = bank()
             for g in passes:
                 nc.tensor.matmul_mx(
@@ -276,109 +234,77 @@ def tile_material_requirements_planning_s9_kernel(tc, orders, inv_words, inv_sca
                 )
             return acc
 
-        def add_and_store(i, acc, s0=0, s1=S, queue=None):
-            res = work.tile([P, s1 - s0], F32, name="res", bufs=RESB)
+        def add_and_store(i, acc, s0=0, s1=S, queue=nc.sync):
+            res = work.tile([P, s1 - s0], F32, name="res", bufs=9)
             nc.vector.tensor_tensor(out=res[:], in0=acc[:, 0 : s1 - s0], in1=con_sb[:, s0:s1], op=ADD)
-            (queue or nc.sync).dma_start(out=out[i * P : (i + 1) * P, s0:s1], in_=res[:])
+            queue.dma_start(out=out[i * P : (i + 1) * P, s0:s1], in_=res[:])
 
-        def clear_plane(h, engine):
-            engine.memset(planes[h][:].rearrange("p g n -> p (g n)").bitcast(I32), 0)
+        calls = {
+            "o": load_orders, "i": load_inv, "c": load_scales, "s": load_shares,
+            "a": lambda i: load_stock(i, 0, HALF), "b": lambda i: load_stock(i, HALF, C), "p": load_stock_pair,
+            "q": lambda i: load_stock(i, 0, N), "r": lambda i: load_stock(i, N, HALF),
+            "O": quantize_orders, "A": lambda i: quantize_net(i, 0), "B": lambda i: quantize_net(i, 1),
+            "R": lambda i: relu(i, 0),
+            "W": quantize_shares, "G": interleave_shares, "Z": clear_plane,
+            "V": lambda i: sort_orders(i, nc.vector.tensor_copy), "S": lambda i: sort_orders(i, nc.scalar.copy),
+        }
 
-        def warm_operands():
-            nc.vector.memset(planes[-1][:, 0, 0:N].bitcast(I32), 0)
-            nc.vector.memset(inv_sb[G2 - 1][:, 0, :].bitcast(I32), 0)
-            nc.vector.memset(ord_codes[MT - 1][:, 0:P], 0)
-
-        def warm_passes(n):
-            release()
-            acc = bank()
-            for j in range(n):
-                nc.tensor.matmul_mx(
-                    out=acc[:],
-                    lhsT=ord_codes[MT - 1][:, 0:P].bitcast(E4M3X4),
-                    lhsT_scale=planes[-1][:, 0, 0:P],
-                    rhs=inv_sb[G2 - 1][:, 0, :].bitcast(E2M1X4),
-                    rhs_scale=planes[-1][:, 0, 0:N],
-                    start=True,
-                    stop=True,
-                )
+        def do(text):
+            for x in text.split():
+                calls[x[0]](int(x[1]))
 
         make_identity(nc, ident[:])
-        if WARM1:
-            warm_operands()
-        for h in range(len(PIECES) - 1):
-            clear_plane(h, nc.vector)
-        loads = {
-            "o": load_orders, "i": load_inv, "c": load_scales, "s": load_shares, "k": load_stock,
-            "a": lambda i: load_stock(i, 0, HALF), "b": lambda i: load_stock(i, HALF, C),
-        }
-        load_orders(0)
-        for x in LOADS.split()[:EARLY]:
-            loads[x[0]](int(x[1]))
-
-        if WARM1:
-            warm_passes(WARM1)
+        do(CLEAR_FIRST)
+        do(FIRST_LOADS)
         new_og(0)
         for g in range(G1):
-            orders_half(0, g, nc.scalar.copy)
-        for x in range(1, HEAD):
-            sort_orders(x, nc.vector.tensor_copy)
-            turn_sorted_by_pass(x)
-        for x in range(HEAD):
+            turn_unsorted_pass(0, g)
+        for i in range(1, HEAD):
+            sort_orders(i, nc.vector.tensor_copy)
+            turn_orders(i, 2)
+        for i in range(HEAD):
             for g in range(G1):
-                quantize_orders(x, g, g + 1)
-        clear_plane(len(PIECES) - 1, nc.vector)
-        for x in LOADS.split()[EARLY:]:
-            loads[x[0]](int(x[1]))
+                quantize_orders(i, g, g + 1)
+        do(CLEAR_LATER)
+        do(LOADS)
         nc.sync.dma_start(out=con_sb[:], in_=contract.partition_broadcast(P))
-        groups = [(i, c) for b in BLOCKS for c in range(2) for i in b] + [(i, c) for i in range(MT) for c in range(2, 4)]
-        halves = [(int(x[1]), "ab".index(x[0])) for x in HALVES.split()]
+
+        groups = FIRST_GROUPS + [(i, c) for h in range(2) for i in range(MT) for c in (2 * h, 2 * h + 1) if (i, c) not in FIRST_GROUPS]
+        subs = FIRST_SUBS + [x for x in groups if x not in FIRST_SUBS]
+        turns = [("o" if x[0] == "o" else "ab".index(x[0]), int(x[1])) for x in TURNS.split()]
         done = []
 
-        def subtract_up_to(j):
-            while len(done) < j:
-                subtract_stock(*groups[len(done)])
+        def subtract_ready(made):
+            while len(done) < len(subs) and subs[len(done)] in made:
+                subtract_stock(*subs[len(done)])
                 done.append(1)
-                for x in AFTER_SUB.get(len(done), "").split():
-                    calls[x[0]](int(x[1]))
+                do(AFTER_SUB.get(len(done), ""))
 
-        def window(g):
-            quantize_shares(g)
-            if g + 1 < G2:
-                interleave_shares(g + 1)
+        def run(n):
+            for kind, i in turns[:n]:
+                if kind == "o":
+                    turn_orders(i, 1)
+                else:
+                    turn_net(i, kind)
+            turns[:n] = []
 
-        calls = {"o": quantize_orders, "a": lambda i: quantize_net(i, 0), "b": lambda i: quantize_net(i, 1), "w": quantize_shares, "x": interleave_on_scalar, "s": lambda i: sort_orders(i, nc.vector.tensor_copy), "g": interleave_shares, "p": lambda i: quantize_orders(i, 0, 1), "q": lambda i: quantize_orders(i, 1, 2)}
-        for x in SORT_AFTER.get(0, ()):
-            sort_orders(x, nc.scalar.copy)
-        taken = 0
+        do(SORTS.get(0, ""))
         for j, (i, c) in enumerate(groups):
-            subtract_up_to(j - LAG)
-            first_product(i, c)
+            if j >= FIRST_SUB_AT:
+                subtract_ready(groups[: j - LAG])
+            first_product(i, c, j < HELD)
             if j + 1 in RUNS:
-                tiles, nh = RUNS[j + 1]
-                for x in tiles:
-                    turn_sorted(x)
-                for n, h in halves[taken : taken + nh]:
-                    turn_net(n, h)
-                taken = taken + nh
-                for x in SORT_AFTER.get(j + 1, ()):
-                    sort_orders(x, nc.scalar.copy)
-                for x in AFTER_RUN.get(j + 1, "").split():
-                    calls[x[0]](int(x[1]))
-        subtract_up_to(len(groups))
-        for n in range(0, MT - 2):
+                run(3)
+                ring.extend(held)
+                held.clear()
+                do(SORTS.get(j + 1, ""))
+        subtract_ready(groups)
+        for n in range(MT - 2):
             acc = second_product(n)
-            for x in QT.get(n, "").split():
-                calls[x[0]](int(x[1]))
+            do(QT.get(n, ""))
             add_and_store(n, acc)
             if n == LAST_RUN:
-                for x, h in halves[taken:]:
-                    turn_net(x, h)
-                for x in AFTER_LAST.split():
-                    calls[x[0]](int(x[1]))
+                run(3)
+                do(AFTER_LAST)
         for n, s0, s1, q in ((6, 0, 256, nc.sync), (6, 256, 512, nc.sync), (7, 0, 256, nc.sync), (7, 256, 384, nc.scalar), (7, 384, 512, nc.sync)):
-            acc = second_product(n, s0, s1)
-            if (n, s0) == (6, 0):
-                for x in QT.get(6, "").split():
-                    calls[x[0]](int(x[1]))
-            add_and_store(n, acc, s0, s1, q)
+            add_and_store(n, second_product(n, s0, s1), s0, s1, q)

from contextlib import ExitStack

import concourse.mybir as mybir
from concourse.masks import make_identity

M, K1, C, S = 1024, 1024, 2048, 512
FLOPS = 2 * M * K1 * C + 2 * M * C * S

F32 = mybir.dt.float32
BF16 = mybir.dt.bfloat16
I32 = mybir.dt.int32
U32 = mybir.dt.uint32
U8 = mybir.dt.uint8
E4M3X4 = mybir.dt.float8_e4m3fn_x4
E5M2X4 = mybir.dt.float8_e5m2_x4
E2M1X4 = mybir.dt.float4_e2m1fn_x4
SUB = mybir.AluOpType.subtract
ADD = mybir.AluOpType.add
MULT = mybir.AluOpType.mult
RELU = mybir.ActivationFunctionType.Relu

P = 128
KP = 512
N = 512
MT = M // P
G1 = K1 // KP
G2 = C // KP
HALF = C // 2
BANKS = 8
PIECES = ((0, 1), (1, 2), (2, 4))
AT_MOVING_CODES, AT_STILL_CODES, AT_MOVING_SCALES, AT_STILL_SCALES = 0, 128, 128, 128
HEAD = 3
GATE_TILE = 5
LAG = 1
CLEAR_FIRST = "Z0 Z1"
CLEAR_LATER = "Z2"
FIRST_LOADS = "o0 o1 o2 i0 c0"
LOADS = "o3 o4 o5 i1 c1 a0 a1 a2 s0 o6 o7 a3 a4 a5 s1 a6 i2 c2 a7 i3 b0 b1 s2 b2 b3 b4 s3 b5 b6 b7"
FIRST_GROUPS = [(0, 0), (1, 0), (2, 0), (0, 1), (1, 1), (2, 1)]
FIRST_SUBS = []
RUNS = (3, 9, 14, 19, 24, 29)
SORTS = {0: "S3 S4 S5", 3: "S6 S7"}
AFTER_SUB = {2: "O3", 3: "O4 O5 G0", 9: "O6 O7 W0 G1", 15: "A0 W1 G2", 21: "A1 W2 G3", 27: "B0 W3", 30: "B1", 32: "A2"}
QT = {0: "B2 A3", 1: "B3 A4", 2: "B4 A6", 3: "B5 A7", 4: "B6", 5: "B7"}
AFTER_LAST = "A5"
LAST_RUN = 1
HELD = 0
LATE_RELU = ()
TURNS = "o3 o4 o5 o6 o7 a0 a1 a2 a3 a4 a5 a6 a7 b0 b1 b2 b3 b4 b5 b6 b7"
FIRST_SUB_AT = 3


def tile_material_requirements_planning_s9_kernel(tc, orders, inv_words, inv_scales, stock, shares, contract, out):
    nc = tc.nc
    with ExitStack() as ctx:
        keep = ctx.enter_context(tc.tile_pool(name="keep", bufs=1))
        work = ctx.enter_context(tc.tile_pool(name="work", bufs=3))
        psum = ctx.enter_context(tc.psum_pool(name="psum", bufs=1))
        ctx.enter_context(tc.manual_schedule())

        def placed(shape, dtype, size, name, start):
            n = shape[1] * (shape[2] if len(shape) == 3 else 1)
            whole = keep.tile([P, n + 256 // size], dtype, name=name, align_bytes=256)
            flat = whole[:, start // size : start // size + n]
            return flat.rearrange("p (g n) -> p g n", g=shape[1]) if len(shape) == 3 else flat

        ident = keep.tile([P, P], F32, name="ident")
        planes = [placed([P, G1, (b - a) * N], U8, 1, "planes%d" % a, AT_MOVING_SCALES) for a, b in PIECES]
        inv_sb = [placed([P, G1, 2 * N], U8, 1, "inv%d" % c, AT_MOVING_CODES) for c in range(G2)]
        ord_sb = [keep.tile([P, K1], BF16, name="ord%d" % i, align_bytes=64) for i in range(MT)]
        stk_first = [keep.tile([P, HALF], BF16, name="stka%d" % i, align_bytes=64) for i in range(MT)]
        stk_pair = [keep.tile([P, 2 * HALF], BF16, name="stkb%d" % j, align_bytes=64) for j in range(MT // 2)]
        stk = {}
        for i in range(MT):
            stk[i, 0] = stk_first[i][:]
            stk[i, 1] = stk_pair[i // 2][:, i % 2 * HALF : (i % 2 + 1) * HALF]
        sh_raw = [keep.tile([P, 4, S], BF16, name="shr%d" % g, align_bytes=64) for g in range(G2)]
        sh_codes = [placed([P, S], U32, 4, "shc%d" % g, AT_MOVING_CODES) for g in range(G2)]
        sh_scales = [placed([P, S], U8, 1, "shs%d" % g, AT_MOVING_SCALES) for g in range(G2)]
        ord_codes = [placed([P, G1 * P], U32, 4, "oc%d" % i, AT_STILL_CODES) for i in range(MT)]
        ord_scales = [placed([P, G1 * P], U8, 1, "os%d" % i, AT_STILL_SCALES) for i in range(MT)]
        net_codes = [placed([P, G2 * P], U32, 4, "nc%d" % i, AT_STILL_CODES) for i in range(MT)]
        net_scales = [placed([P, G2 * P], U8, 1, "ns%d" % i, AT_STILL_SCALES) for i in range(MT)]
        con_sb = keep.tile([P, S], BF16, name="con", align_bytes=64)
        sh_grp, og, nets, ng, srt, acc1, turned = {}, {}, {}, {}, {}, {}, {}
        ring, held = list(range(BANKS)), []

        def bank(hold=False):
            b = ring.pop(0)
            (held if hold else ring).append(b)
            return psum.tile([P, N], F32, name="bank%d" % b)

        def load_orders(i):
            nc.sync.dma_start(out=ord_sb[i][:], in_=orders[i * P : (i + 1) * P, :])

        def load_stock(i, c0, c1):
            nc.sync.dma_start(out=stk[i, c0 // HALF][:, c0 % HALF : c0 % HALF + c1 - c0], in_=stock[i * P : (i + 1) * P, c0:c1])

        def load_stock_pair(j):
            nc.sync.dma_start(
                out=stk_pair[j][:].rearrange("p (t c) -> p t c", t=2),
                in_=stock[2 * j * P : 2 * (j + 1) * P, HALF:C].rearrange("(t p) c -> p t c", t=2),
            )

        def load_inv(c):
            nc.sync.dma_start(
                out=inv_sb[c][:].bitcast(I32),
                in_=inv_words.rearrange("g p b -> p g b")[:, :, 2 * N * c : 2 * N * (c + 1)].bitcast(I32),
            )

        def load_scales(h):
            rows = inv_scales.rearrange("g (q r) n -> r q g n", r=4)
            for r in range(4):
                nc.sync.dma_start(out=planes[h][r:P:32, :, :].bitcast(I32), in_=rows[r][:, :, PIECES[h][0] * N : PIECES[h][1] * N].bitcast(I32))

        def load_shares(g):
            nc.sync.dma_start(out=sh_raw[g][:], in_=shares[g * KP : (g + 1) * KP, :].rearrange("(p j) s -> p j s", j=4))

        def clear_plane(h):
            nc.vector.memset(planes[h][:].rearrange("p g n -> p (g n)").bitcast(I32), 0)

        def new_og(i):
            if i == GATE_TILE:
                og[i] = work.tile([P, K1], BF16, name="shg", align_bytes=64, bufs=1)
            else:
                og[i] = work.tile([P, K1], BF16, name="og", align_bytes=64, bufs=4)

        def turn_unsorted_pass(i, g):
            t = bank()
            words = ord_sb[i][:].bitcast(F32)
            for u in range(2):
                nc.tensor.transpose(t[:, u * P : (u + 1) * P], words[:, 256 * g + u : 256 * (g + 1) : 2], ident[:])
            nc.scalar.copy(
                out=og[i][:, g * KP : (g + 1) * KP].bitcast(F32).rearrange("p (m u) -> p m u", u=2),
                in_=t[:, 0 : 2 * P].rearrange("p (u m) -> p m u", u=2),
            )

        def sort_orders(i, engine_copy):
            srt[i] = work.tile([P, K1 // 2], F32, name="srt", align_bytes=64, bufs=4)
            engine_copy(
                out=srt[i][:].rearrange("m (u x) -> m u x", u=2),
                in_=ord_sb[i][:].bitcast(F32).rearrange("m (x u) -> m u x", u=2),
            )

        def turn_orders(i, pieces):
            new_og(i)
            t = bank()
            for j in range(4):
                nc.tensor.transpose(t[:, j * P : (j + 1) * P], srt[i][:, j * P : (j + 1) * P], ident[:])
            w = 2 * P // pieces
            for j in range(pieces):
                nc.scalar.copy(
                    out=og[i][:].bitcast(F32).rearrange("p (x u) -> p x u", u=2)[:, j * w : (j + 1) * w, :],
                    in_=t[:].rearrange("p (u x) -> p x u", u=2)[:, j * w : (j + 1) * w, :],
                )

        def quantize_orders(i, a=0, b=G1):
            nc.vector.quantize_mx(
                out=ord_codes[i][:, a * P : b * P].bitcast(E4M3X4),
                scales=ord_scales[i][:, a * P : b * P],
                in_=og[i][:, a * KP : b * KP],
            )

        def first_product(i, c, hold):
            h = [j for j, (a, b) in enumerate(PIECES) if a <= c < b][0]
            acc1[i, c] = bank(hold)
            for g in range(G1):
                nc.tensor.matmul_mx(
                    out=acc1[i, c][:],
                    lhsT=ord_codes[i][:, g * P : (g + 1) * P].bitcast(E4M3X4),
                    lhsT_scale=ord_scales[i][:, g * P : (g + 1) * P],
                    rhs=inv_sb[c][:, g, :].bitcast(E2M1X4),
                    rhs_scale=planes[h][:, g, (c - PIECES[h][0]) * N : (c - PIECES[h][0] + 1) * N],
                    start=(g == 0),
                    stop=(g == G1 - 1),
                )

        def subtract_stock(i, c):
            if c % 2 == 0:
                nets[i, c // 2] = work.tile([P, HALF], BF16, name="net", align_bytes=64, bufs=8)
            nc.vector.tensor_tensor(
                out=nets[i, c // 2][:, c % 2 * N : (c % 2 + 1) * N].rearrange("m (u p e) -> m u p e", u=2, e=2),
                in0=acc1[i, c][:].rearrange("m (p u e) -> m u p e", u=2, e=2),
                in1=stk[i, c // 2][:, c % 2 * N : (c % 2 + 1) * N].rearrange("m (p u e) -> m u p e", u=2, e=2),
                op=SUB,
            )

        def turn_net(i, h):
            t = bank()
            words = nets[i, h][:].bitcast(F32)
            for cl in range(2):
                for u in range(2):
                    nc.tensor.transpose(t[:, u * 256 + cl * P : u * 256 + (cl + 1) * P], words[:, 256 * cl + P * u : 256 * cl + P * (u + 1)], ident[:])
            ng[i, h] = work.tile([P, HALF], BF16, name="ng", align_bytes=64, bufs=16)
            turned[i, h] = t
            if (i, h) not in LATE_RELU:
                relu(i, h)

        def relu(i, h):
            nc.scalar.activation(out=relu_out(i, h), in_=relu_in(i, h), func=RELU)

        def relu_out(i, h):
            return ng[i, h][:].rearrange("p (x u e) -> p x u e", u=2, e=2)

        def relu_in(i, h):
            return turned[i, h][:].bitcast(BF16).rearrange("p (u x e) -> p x u e", u=2, e=2)

        def quantize_net(i, h):
            nc.vector.quantize_mx(
                out=net_codes[i][:, 2 * h * P : 2 * (h + 1) * P].bitcast(E5M2X4),
                scales=net_scales[i][:, 2 * h * P : 2 * (h + 1) * P],
                in_=ng[i, h][:],
            )

        def interleave_shares(g):
            sh_grp[g] = work.tile([P, S, 4], BF16, name="shg", align_bytes=64, bufs=1)
            nc.gpsimd.tensor_scalar(out=sh_grp[g][:], in0=sh_raw[g][:].rearrange("p t s -> p s t"), scalar1=1.0, scalar2=0.0, op0=MULT, op1=ADD)

        def quantize_shares(g):
            nc.vector.quantize_mx(out=sh_codes[g][:].bitcast(E4M3X4), scales=sh_scales[g][:], in_=sh_grp[g][:].rearrange("p s t -> p (s t)"))

        def second_product(i, s0=0, s1=S, passes=range(G2), acc=None):
            if acc is None:
                acc = bank()
            for g in passes:
                nc.tensor.matmul_mx(
                    out=acc[:, 0 : s1 - s0],
                    lhsT=net_codes[i][:, g * P : (g + 1) * P].bitcast(E5M2X4),
                    lhsT_scale=net_scales[i][:, g * P : (g + 1) * P],
                    rhs=sh_codes[g][:, s0:s1].bitcast(E4M3X4),
                    rhs_scale=sh_scales[g][:, s0:s1],
                    start=(g == 0),
                    stop=(g == G2 - 1),
                )
            return acc

        def add_and_store(i, acc, s0=0, s1=S, queue=nc.sync):
            res = work.tile([P, s1 - s0], F32, name="res", bufs=9)
            nc.vector.tensor_tensor(out=res[:], in0=acc[:, 0 : s1 - s0], in1=con_sb[:, s0:s1], op=ADD)
            queue.dma_start(out=out[i * P : (i + 1) * P, s0:s1], in_=res[:])

        calls = {
            "o": load_orders, "i": load_inv, "c": load_scales, "s": load_shares,
            "a": lambda i: load_stock(i, 0, HALF), "b": lambda i: load_stock(i, HALF, C), "p": load_stock_pair,
            "q": lambda i: load_stock(i, 0, N), "r": lambda i: load_stock(i, N, HALF),
            "O": quantize_orders, "A": lambda i: quantize_net(i, 0), "B": lambda i: quantize_net(i, 1),
            "R": lambda i: relu(i, 0),
            "W": quantize_shares, "G": interleave_shares, "Z": clear_plane,
            "V": lambda i: sort_orders(i, nc.vector.tensor_copy), "S": lambda i: sort_orders(i, nc.scalar.copy),
        }

        def do(text):
            for x in text.split():
                calls[x[0]](int(x[1]))

        make_identity(nc, ident[:])
        do(CLEAR_FIRST)
        do(FIRST_LOADS)
        new_og(0)
        for g in range(G1):
            turn_unsorted_pass(0, g)
        for i in range(1, HEAD):
            sort_orders(i, nc.vector.tensor_copy)
            turn_orders(i, 2)
        for i in range(HEAD):
            for g in range(G1):
                quantize_orders(i, g, g + 1)
        do(CLEAR_LATER)
        do(LOADS)
        nc.sync.dma_start(out=con_sb[:], in_=contract.partition_broadcast(P))

        groups = FIRST_GROUPS + [(i, c) for h in range(2) for i in range(MT) for c in (2 * h, 2 * h + 1) if (i, c) not in FIRST_GROUPS]
        subs = FIRST_SUBS + [x for x in groups if x not in FIRST_SUBS]
        turns = [("o" if x[0] == "o" else "ab".index(x[0]), int(x[1])) for x in TURNS.split()]
        done = []

        def subtract_ready(made):
            while len(done) < len(subs) and subs[len(done)] in made:
                subtract_stock(*subs[len(done)])
                done.append(1)
                do(AFTER_SUB.get(len(done), ""))

        def run(n):
            for kind, i in turns[:n]:
                if kind == "o":
                    turn_orders(i, 1)
                else:
                    turn_net(i, kind)
            turns[:n] = []

        do(SORTS.get(0, ""))
        for j, (i, c) in enumerate(groups):
            if j >= FIRST_SUB_AT:
                subtract_ready(groups[: j - LAG])
            first_product(i, c, j < HELD)
            if j + 1 in RUNS:
                run(3)
                ring.extend(held)
                held.clear()
                do(SORTS.get(j + 1, ""))
        subtract_ready(groups)
        for n in range(MT - 2):
            acc = second_product(n)
            do(QT.get(n, ""))
            add_and_store(n, acc)
            if n == LAST_RUN:
                run(3)
                do(AFTER_LAST)
        for n, s0, s1, q in ((6, 0, 256, nc.sync), (6, 256, 512, nc.sync), (7, 0, 256, nc.sync), (7, 256, 384, nc.scalar), (7, 384, 512, nc.sync)):
            add_and_store(n, second_product(n, s0, s1), s0, s1, q)
